import numpy as np
import ml_dtypes


def mxq(x, axis, fmt="e4m3"):
    dtype, down = {"e4m3": (ml_dtypes.float8_e4m3fn, 7), "e5m2": (ml_dtypes.float8_e5m2, 14)}[fmt]
    v = np.moveaxis(np.asarray(x, np.float32).astype(ml_dtypes.bfloat16).astype(np.float64), axis, -1)
    blocks = v.reshape(v.shape[:-1] + (-1, 32))
    amax = np.abs(blocks).max(-1, keepdims=True)
    byte = np.maximum(np.where(amax > 0, np.frexp(amax)[1] - 1 + 127, 0) - down, 1)
    scale = np.exp2(byte - 127.0)
    codes = (blocks / scale).astype(np.float32).astype(dtype).astype(np.float64)
    return np.moveaxis((codes * scale).reshape(v.shape), -1, axis)


WIDE = False


def mx_kscale(k):
    if not WIDE:
        return np.ones(k)
    levels = np.array([10, -10, 5, -5, 0])
    if k % 512:
        return np.exp2(np.random.permutation(np.resize(levels, k // 32))).repeat(32)
    a = np.empty((k // 512, 16))
    for p in range(k // 512):
        a[p, :8] = np.random.permutation(np.resize(levels, 8))
        for g in range(8):
            far = levels[np.abs(levels - a[p, g]) >= 10]
            a[p, g + 8] = far[np.random.randint(len(far))]
    return np.exp2(a.ravel()).repeat(32)


def f64(x):
    return np.asarray(x).astype(np.float64)


def striped(idx):
    return np.tile(idx.reshape(-1, 16).T, (8, 1)).astype(np.uint16)


def unstriped(offs):
    return offs[:16].T.reshape(-1).astype(np.int64)


def sigmoid(v):
    return 1.0 / (1.0 + np.exp(-np.maximum(v, -700.0)))

def planes(y):
    n, m = y.shape
    v = y.astype(np.float32).astype(ml_dtypes.bfloat16).astype(np.float64).reshape(n // 32, 32, m)
    top = np.abs(v).max(1)
    byte = np.clip(np.where(top > 0, np.frexp(top)[1] - 1 + 127 - 7, 1), 1, 254)
    codes = (v * np.exp2(127.0 - byte)[:, None, :]).reshape(n, m).astype(np.float32).astype(ml_dtypes.float8_e4m3fn).view(np.uint8)
    words = codes.reshape(n // 512, 128, 4, m).transpose(0, 1, 3, 2)
    return np.ascontiguousarray(words), np.ascontiguousarray(byte.astype(np.uint8).reshape(n // 512, 16, m))


K, T, S, V, N = 512, 1024, 512, 128, 512


def setup_inputs():
    n = np.random.standard_normal
    s = mx_kscale(K)[:, None]
    return {
        "xT": (n((K, T)) * s).astype(np.float32),
        "w1": (n((K, N)) / np.sqrt(K) / s).astype(np.float32),
        "offs": striped(np.random.permutation(T)[:S]),
    }


def reference(xT, w1, offs):
    xq = mxq(f64(xT)[:, unstriped(offs)], 0, "e4m3")
    y = sigmoid(mxq(f64(w1), 0, "e4m3").T @ xq)
    out_0 = ((y[:, :V] * y[:, V:2 * V]) * y[:, 2 * V:3 * V]) * y[:, 3 * V:4 * V]
    return (out_0,) + planes(out_0)

@@ -1,0 +1,135 @@
+from contextlib import ExitStack
+
+import concourse.mybir as mybir
+
+K, T, S, V, N = 512, 1024, 512, 128, 512
+D = S // V
+P = 128
+PACK = 4
+FLOPS = 2 * K * N * S
+
+F32 = mybir.dt.float32
+BF16 = mybir.dt.bfloat16
+I32 = mybir.dt.int32
+U32 = mybir.dt.uint32
+U16 = mybir.dt.uint16
+U8 = mybir.dt.uint8
+FP8X4 = mybir.dt.float8_e4m3fn_x4
+SIGMOID = mybir.ActivationFunctionType.Sigmoid
+MULT = mybir.AluOpType.mult
+COLS = V // 16
+W_CHUNKS = ((0, 32), (32, 64), (64, 96), (96, 128))
+W_VECTOR = 20
+
+
+def tile_picked_andpool_none_lo_kernel(tc, xT, w1, offs, out_0, out_1, out_2):
+    nc = tc.nc
+    with ExitStack() as ctx:
+        keep = ctx.enter_context(tc.tile_pool(name="keep", bufs=1))
+        psum = ctx.enter_context(tc.psum_pool(name="psum", bufs=1))
+
+        warm_in = keep.tile([P, 1], F32, name="warm_in")
+        warm_out = keep.tile([P, 1], F32, name="warm_out")
+        nc.vector.memset(warm_in[:], 0.0)
+        nc.scalar.activation(warm_out[:], warm_in[:], SIGMOID)
+
+        x_rows = xT.rearrange("(p j) t -> p j t", j=PACK)
+        w_rows = w1.rearrange("(p j) c -> p j c", j=PACK)
+        offsets = keep.tile([P, S // 16], U16, name="offsets")
+        planes = [keep.tile([P, T], F32, name="plane%d" % j) for j in range(PACK)]
+        w_raw = [keep.tile([P, PACK, PACK * (hi - lo)], F32, name="w_raw%d" % lo) for lo, hi in W_CHUNKS]
+
+        nc.sync.dma_start(planes[0][:], x_rows[:, 0, :])
+        nc.sync.dma_start(offsets[:], offs)
+        for j in range(1, PACK):
+            nc.sync.dma_start(planes[j][:], x_rows[:, j, :])
+        for raw, (lo, hi) in zip(w_raw, W_CHUNKS):
+            nc.sync.dma_start(raw[:], w_rows[:, :, PACK * lo : PACK * hi])
+
+        x_grouped = keep.tile([P, S, PACK], BF16, name="x_grouped", align_bytes=64)
+        w_grouped = keep.tile([P, PACK, P, PACK], BF16, name="w_grouped", align_bytes=64)
+        x_first = keep.tile([P, 2, S], BF16, name="x_first", align_bytes=64)
+        for j in range(2):
+            nc.vector.tensor_copy(x_first[:, j, :], planes[j][:].indirect(offsets[:]))
+        nc.scalar.copy(x_grouped[:, :, 0:2], x_first[:].rearrange("p j n -> p n j"))
+        for j in range(2, PACK):
+            nc.vector.tensor_copy(x_grouped[:, :, j], planes[j][:].indirect(offsets[:]))
+
+        def w_views(c, first, last):
+            lo = W_CHUNKS[c][0]
+            dst = w_grouped[:, :, first:last, :].rearrange("p t m j -> p m t j")
+            src = w_raw[c][:].rearrange("p j (m t) -> p m t j", t=PACK)[:, first - lo : last - lo, :, :]
+            return dst, src
+
+        HALF = S // 2
+        x_codes = [keep.tile([P, HALF], U32, name="x_codes%d" % h, align_bytes=64) for h in range(2)]
+        x_scales = [keep.tile([P, HALF], U8, name="x_scales%d" % h, align_bytes=64) for h in range(2)]
+        for h in range(2):
+            nc.vector.quantize_mx(
+                out=x_codes[h][:].bitcast(FP8X4),
+                scales=x_scales[h][:],
+                in_=x_grouped[:, h * HALF : (h + 1) * HALF, :].rearrange("p n j -> p (n j)"),
+            )
+        for c, (lo, hi) in enumerate(W_CHUNKS[:-1]):
+            nc.scalar.copy(*w_views(c, lo, hi))
+        c = len(W_CHUNKS) - 1
+        nc.scalar.copy(*w_views(c, W_CHUNKS[c][0], P - W_VECTOR))
+        nc.vector.tensor_copy(*w_views(c, P - W_VECTOR, P))
+
+        w_codes = [keep.tile([P, P], U32, name="w_codes%d" % t, align_bytes=64) for t in range(PACK)]
+        w_scales = [keep.tile([P, P], U8, name="w_scales%d" % t, align_bytes=64) for t in range(PACK)]
+        for t in range(PACK):
+            nc.vector.quantize_mx(
+                out=w_codes[t][:].bitcast(FP8X4),
+                scales=w_scales[t][:],
+                in_=w_grouped[:, t, :, :].rearrange("p m j -> p (m j)"),
+            )
+
+        def products(u, h):
+            bank = psum.tile([P, 2, 2, V], F32, name="bank%d%d" % (u, h))
+            for e in range(2):
+                t = 2 * u + e
+                nc.tensor.matmul_mx(
+                    out=bank[:, e, :, :].rearrange("p d v -> p (d v)"),
+                    lhsT=w_codes[t][:].bitcast(FP8X4),
+                    lhsT_scale=w_scales[t][:],
+                    rhs=x_codes[h][:].bitcast(FP8X4),
+                    rhs_scale=x_scales[h][:],
+                    start=True,
+                    stop=True,
+                )
+            return bank
+
+        running = {}
+        for u in range(2):
+            bank = products(u, 0)
+            truth = keep.tile([P, 2, 2, V], F32, name="truth_lead%d" % u)
+            nc.scalar.activation(truth[:], bank[:], SIGMOID)
+            running[u] = keep.tile([P, 2, V], F32, name="two%d" % u)
+            nc.vector.tensor_tensor(running[u][:], truth[:, :, 0, :], truth[:, :, 1, :], MULT)
+        banks = {u: products(u, 1) for u in (0, 1)}
+        y_grouped = keep.tile([P, V, PACK], BF16, name="y_grouped", align_bytes=64)
+        out_rows = out_0.rearrange("(p t) v -> p t v", t=PACK)
+        for u, e in ((0, 0), (1, 0), (0, 1), (1, 1)):
+            truth = keep.tile([P, 2, V], F32, name="truth%d%d" % (u, e))
+            nc.scalar.activation(truth[:], banks[u][:, :, e, :], SIGMOID)
+            product = keep.tile([P, 2, V], F32, name="product%d%d" % (u, e))
+            nc.vector.tensor_tensor(product[:], running[u][:], truth[:], MULT)
+            running[u] = product
+        for u in range(2):
+            nc.sync.dma_start(out_rows[:, 2 * u : 2 * u + 2, :], running[u][:])
+        for u in range(2):
+            nc.vector.tensor_copy(y_grouped[:, :, 2 * u : 2 * u + 2], running[u][:].rearrange("p t v -> p v t"))
+
+        y_codes = keep.tile([P, V], U32, name="y_codes", align_bytes=64)
+        y_scales = keep.tile([P, V], U8, name="y_scales", align_bytes=64)
+        nc.vector.quantize_mx(
+            out=y_codes[:].bitcast(FP8X4),
+            scales=y_scales[:],
+            in_=y_grouped[:].rearrange("p v t -> p (v t)"),
+        )
+        nc.sync.dma_start(out_1.rearrange("z l c r -> (z l) (c r)").bitcast(I32), y_codes[:].bitcast(I32))
+        scale_rows = out_2.rearrange("z q c -> (z q) c").bitcast(I32)
+        for q in range(4):
+            queue = nc.sync if q % 2 == 0 else nc.scalar
+            queue.dma_start(scale_rows[4 * q : 4 * q + 4, :], y_scales[32 * q : 32 * q + 4, :].bitcast(I32))

@@ -18,8 +18,8 @@ FP8X4 = mybir.dt.float8_e4m3fn_x4
 SIGMOID = mybir.ActivationFunctionType.Sigmoid
 MULT = mybir.AluOpType.mult
 COLS = V // 16
-W_CHUNKS = ((0, 32), (32, 64), (64, 96), (96, 128))
-W_VECTOR = 20
+W_CHUNKS = ((0, 64), (64, 128))
+W_VECTOR = 42
 
 
 def tile_picked_andpool_none_lo_kernel(tc, xT, w1, offs, out_0, out_1, out_2):
@@ -37,7 +37,7 @@ def tile_picked_andpool_none_lo_kernel(tc, xT, w1, offs, out_0, out_1, out_2):
         w_rows = w1.rearrange("(p j) c -> p j c", j=PACK)
         offsets = keep.tile([P, S // 16], U16, name="offsets")
         planes = [keep.tile([P, T], F32, name="plane%d" % j) for j in range(PACK)]
-        w_raw = [keep.tile([P, PACK, PACK * (hi - lo)], F32, name="w_raw%d" % lo) for lo, hi in W_CHUNKS]
+        w_raw = [keep.tile([P, PACK, PACK * (hi - lo)], F32, name="w_raw%d" % lo, tag="w_raw%d" % lo, align_bytes=64) for lo, hi in W_CHUNKS]
 
         nc.sync.dma_start(planes[0][:], x_rows[:, 0, :])
         nc.sync.dma_start(offsets[:], offs)
@@ -62,19 +62,24 @@ def tile_picked_andpool_none_lo_kernel(tc, xT, w1, offs, out_0, out_1, out_2):
             return dst, src
 
         HALF = S // 2
-        x_codes = [keep.tile([P, HALF], U32, name="x_codes%d" % h, align_bytes=64) for h in range(2)]
-        x_scales = [keep.tile([P, HALF], U8, name="x_scales%d" % h, align_bytes=64) for h in range(2)]
-        for h in range(2):
+
+        def quantize_half(h, tag):
+            codes = keep.tile([P, HALF], U32, name="x_codes%d" % h, tag=tag, align_bytes=64)
+            scales = keep.tile([P, HALF], U8, name="x_scales%d" % h, align_bytes=64)
             nc.vector.quantize_mx(
-                out=x_codes[h][:].bitcast(FP8X4),
-                scales=x_scales[h][:],
+                out=codes[:].bitcast(FP8X4),
+                scales=scales[:],
                 in_=x_grouped[:, h * HALF : (h + 1) * HALF, :].rearrange("p n j -> p (n j)"),
             )
+            return codes, scales
+
+        x_halves = [quantize_half(0, "x_codes0")]
         for c, (lo, hi) in enumerate(W_CHUNKS[:-1]):
             nc.scalar.copy(*w_views(c, lo, hi))
         c = len(W_CHUNKS) - 1
         nc.scalar.copy(*w_views(c, W_CHUNKS[c][0], P - W_VECTOR))
         nc.vector.tensor_copy(*w_views(c, P - W_VECTOR, P))
+        x_halves.append(quantize_half(1, "w_raw0"))
 
         w_codes = [keep.tile([P, P], U32, name="w_codes%d" % t, align_bytes=64) for t in range(PACK)]
         w_scales = [keep.tile([P, P], U8, name="w_scales%d" % t, align_bytes=64) for t in range(PACK)]
@@ -85,41 +90,46 @@ def tile_picked_andpool_none_lo_kernel(tc, xT, w1, offs, out_0, out_1, out_2):
                 in_=w_grouped[:, t, :, :].rearrange("p m j -> p (m j)"),
             )
 
-        def products(u, h):
-            bank = psum.tile([P, 2, 2, V], F32, name="bank%d%d" % (u, h))
+        def truth_values(u, d):
+            codes, scales = x_halves[d // 2]
+            cols = slice((d % 2) * V, (d % 2 + 1) * V)
+            bank = psum.tile([P, 2, V], F32, name="bank%d%d" % (u, d))
             for e in range(2):
                 t = 2 * u + e
                 nc.tensor.matmul_mx(
-                    out=bank[:, e, :, :].rearrange("p d v -> p (d v)"),
+                    out=bank[:, e, :],
                     lhsT=w_codes[t][:].bitcast(FP8X4),
                     lhsT_scale=w_scales[t][:],
-                    rhs=x_codes[h][:].bitcast(FP8X4),
-                    rhs_scale=x_scales[h][:],
+                    rhs=codes[:, cols].bitcast(FP8X4),
+                    rhs_scale=scales[:, cols],
                     start=True,
                     stop=True,
                 )
-            return bank
-
-        running = {}
-        for u in range(2):
-            bank = products(u, 0)
-            truth = keep.tile([P, 2, 2, V], F32, name="truth_lead%d" % u)
+            truth = keep.tile([P, 2, V], F32, name="truth%d%d" % (u, d))
             nc.scalar.activation(truth[:], bank[:], SIGMOID)
-            running[u] = keep.tile([P, 2, V], F32, name="two%d" % u)
-            nc.vector.tensor_tensor(running[u][:], truth[:, :, 0, :], truth[:, :, 1, :], MULT)
-        banks = {u: products(u, 1) for u in (0, 1)}
+            return truth
+
         y_grouped = keep.tile([P, V, PACK], BF16, name="y_grouped", align_bytes=64)
         out_rows = out_0.rearrange("(p t) v -> p t v", t=PACK)
-        for u, e in ((0, 0), (1, 0), (0, 1), (1, 1)):
-            truth = keep.tile([P, 2, V], F32, name="truth%d%d" % (u, e))
-            nc.scalar.activation(truth[:], banks[u][:, :, e, :], SIGMOID)
-            product = keep.tile([P, 2, V], F32, name="product%d%d" % (u, e))
+        running = {}
+        for u, d in ((0, 0), (0, 1), (1, 0), (1, 1), (0, 2), (1, 2), (0, 3), (1, 3)):
+            truth = truth_values(u, d)
+            if d == 0:
+                running[u] = truth
+                continue
+            if (u, d) == (1, D - 1):
+                nc.vector.tensor_tensor(
+                    y_grouped[:, :, 2:4],
+                    running[u][:].rearrange("p t v -> p v t"),
+                    truth[:].rearrange("p t v -> p v t"),
+                    MULT,
+                )
+            product = keep.tile([P, 2, V], F32, name="product%d%d" % (u, d))
             nc.vector.tensor_tensor(product[:], running[u][:], truth[:], MULT)
             running[u] = product
         for u in range(2):
             nc.sync.dma_start(out_rows[:, 2 * u : 2 * u + 2, :], running[u][:])
-        for u in range(2):
-            nc.vector.tensor_copy(y_grouped[:, :, 2 * u : 2 * u + 2], running[u][:].rearrange("p t v -> p v t"))
+        nc.scalar.copy(y_grouped[:, :, 0:2], running[0][:].rearrange("p t v -> p v t"))
 
         y_codes = keep.tile([P, V], U32, name="y_codes", align_bytes=64)
         y_scales = keep.tile([P, V], U8, name="y_scales", align_bytes=64)

@@ -18,8 +18,8 @@ FP8X4 = mybir.dt.float8_e4m3fn_x4
 SIGMOID = mybir.ActivationFunctionType.Sigmoid
 MULT = mybir.AluOpType.mult
 COLS = V // 16
-W_CHUNKS = ((0, 64), (64, 128))
-W_VECTOR = 42
+W_CHUNKS = ((0, 32), (32, 64), (64, 128))
+W_VECTOR = 40
 
 
 def tile_picked_andpool_none_lo_kernel(tc, xT, w1, offs, out_0, out_1, out_2):
@@ -41,19 +41,42 @@ def tile_picked_andpool_none_lo_kernel(tc, xT, w1, offs, out_0, out_1, out_2):
 
         nc.sync.dma_start(planes[0][:], x_rows[:, 0, :])
         nc.sync.dma_start(offsets[:], offs)
-        for j in range(1, PACK):
-            nc.sync.dma_start(planes[j][:], x_rows[:, j, :])
-        for raw, (lo, hi) in zip(w_raw, W_CHUNKS):
-            nc.sync.dma_start(raw[:], w_rows[:, :, PACK * lo : PACK * hi])
 
-        x_grouped = keep.tile([P, S, PACK], BF16, name="x_grouped", align_bytes=64)
+        def load_w(c):
+            lo, hi = W_CHUNKS[c]
+            nc.sync.dma_start(w_raw[c][:], w_rows[:, :, PACK * lo : PACK * hi])
+
+        for j in range(1, PACK - 1):
+            nc.sync.dma_start(planes[j][:], x_rows[:, j, :])
+        for c in range(1):
+            load_w(c)
+        nc.sync.dma_start(planes[PACK - 1][:], x_rows[:, PACK - 1, :])
+        for c in range(1, len(W_CHUNKS)):
+            load_w(c)
+
         w_grouped = keep.tile([P, PACK, P, PACK], BF16, name="w_grouped", align_bytes=64)
-        x_first = keep.tile([P, 2, S], BF16, name="x_first", align_bytes=64)
+        picked = keep.tile([P, PACK, S], BF16, name="picked", align_bytes=64)
+        HALF = S // 2
+        lead_grouped = keep.tile([P, HALF, PACK], BF16, name="lead_grouped", align_bytes=64)
         for j in range(2):
-            nc.vector.tensor_copy(x_first[:, j, :], planes[j][:].indirect(offsets[:]))
-        nc.scalar.copy(x_grouped[:, :, 0:2], x_first[:].rearrange("p j n -> p n j"))
+            nc.vector.tensor_copy(picked[:, j, :], planes[j][:].indirect(offsets[:]))
+        nc.scalar.copy(lead_grouped[:, :, 0:2], picked[:, 0:2, :HALF].rearrange("p j n -> p n j"))
         for j in range(2, PACK):
-            nc.vector.tensor_copy(x_grouped[:, :, j], planes[j][:].indirect(offsets[:]))
+            nc.vector.tensor_copy(lead_grouped[:, :, j], planes[j][:].indirect(offsets[:, : HALF // 16]))
+            nc.vector.tensor_copy(picked[:, j, HALF:], planes[j][:].indirect(offsets[:, HALF // 16 :]))
+
+        def quantize_entries(grouped, lo, tag):
+            width = grouped.shape[1]
+            codes = keep.tile([P, width], U32, name="x_codes%d" % lo, tag=tag, align_bytes=64)
+            scales = keep.tile([P, width], U8, name="x_scales%d" % lo, align_bytes=64)
+            nc.vector.quantize_mx(
+                out=codes[:].bitcast(FP8X4),
+                scales=scales[:],
+                in_=grouped.rearrange("p n j -> p (n j)"),
+            )
+            return [(codes[:, c : c + V], scales[:, c : c + V]) for c in range(0, width, V)]
+
+        pieces = quantize_entries(lead_grouped[:], 0, "x_codes0")
 
         def w_views(c, first, last):
             lo = W_CHUNKS[c][0]
@@ -61,25 +84,11 @@ def tile_picked_andpool_none_lo_kernel(tc, xT, w1, offs, out_0, out_1, out_2):
             src = w_raw[c][:].rearrange("p j (m t) -> p m t j", t=PACK)[:, first - lo : last - lo, :, :]
             return dst, src
 
-        HALF = S // 2
-
-        def quantize_half(h, tag):
-            codes = keep.tile([P, HALF], U32, name="x_codes%d" % h, tag=tag, align_bytes=64)
-            scales = keep.tile([P, HALF], U8, name="x_scales%d" % h, align_bytes=64)
-            nc.vector.quantize_mx(
-                out=codes[:].bitcast(FP8X4),
-                scales=scales[:],
-                in_=x_grouped[:, h * HALF : (h + 1) * HALF, :].rearrange("p n j -> p (n j)"),
-            )
-            return codes, scales
-
-        x_halves = [quantize_half(0, "x_codes0")]
         for c, (lo, hi) in enumerate(W_CHUNKS[:-1]):
             nc.scalar.copy(*w_views(c, lo, hi))
         c = len(W_CHUNKS) - 1
         nc.scalar.copy(*w_views(c, W_CHUNKS[c][0], P - W_VECTOR))
         nc.vector.tensor_copy(*w_views(c, P - W_VECTOR, P))
-        x_halves.append(quantize_half(1, "w_raw0"))
 
         w_codes = [keep.tile([P, P], U32, name="w_codes%d" % t, align_bytes=64) for t in range(PACK)]
         w_scales = [keep.tile([P, P], U8, name="w_scales%d" % t, align_bytes=64) for t in range(PACK)]
@@ -90,9 +99,17 @@ def tile_picked_andpool_none_lo_kernel(tc, xT, w1, offs, out_0, out_1, out_2):
                 in_=w_grouped[:, t, :, :].rearrange("p m j -> p (m j)"),
             )
 
+        rest_grouped = keep.tile([P, HALF, PACK], BF16, name="rest_grouped", tag="w_raw%d" % W_CHUNKS[-1][0], align_bytes=64)
+        for d, copy in ((2, nc.scalar.copy), (3, nc.vector.tensor_copy)):
+            copy(
+                rest_grouped[:, (d - 2) * V : (d - 1) * V, :].rearrange("p (c i) j -> p c j i", i=4),
+                picked[:, :, d * V : (d + 1) * V].rearrange("p j (c i) -> p c j i", i=4),
+            )
+        for d in (2, 3):
+            pieces = pieces + quantize_entries(rest_grouped[:, (d - 2) * V : (d - 1) * V, :], d * V, "x_codes%d" % (d * V))
+
         def truth_values(u, d):
-            codes, scales = x_halves[d // 2]
-            cols = slice((d % 2) * V, (d % 2 + 1) * V)
+            codes, scales = pieces[d]
             bank = psum.tile([P, 2, V], F32, name="bank%d%d" % (u, d))
             for e in range(2):
                 t = 2 * u + e
@@ -100,8 +117,8 @@ def tile_picked_andpool_none_lo_kernel(tc, xT, w1, offs, out_0, out_1, out_2):
                     out=bank[:, e, :],
                     lhsT=w_codes[t][:].bitcast(FP8X4),
                     lhsT_scale=w_scales[t][:],
-                    rhs=codes[:, cols].bitcast(FP8X4),
-                    rhs_scale=scales[:, cols],
+                    rhs=codes.bitcast(FP8X4),
+                    rhs_scale=scales,
                     start=True,
                     stop=True,
                 )

@@ -18,8 +18,8 @@ FP8X4 = mybir.dt.float8_e4m3fn_x4
 SIGMOID = mybir.ActivationFunctionType.Sigmoid
 MULT = mybir.AluOpType.mult
 COLS = V // 16
-W_CHUNKS = ((0, 32), (32, 64), (64, 128))
-W_VECTOR = 40
+W_CHUNKS = ((0, 64), (64, 128))
+W_VECTOR = 50
 
 
 def tile_picked_andpool_none_lo_kernel(tc, xT, w1, offs, out_0, out_1, out_2):
@@ -48,10 +48,8 @@ def tile_picked_andpool_none_lo_kernel(tc, xT, w1, offs, out_0, out_1, out_2):
 
         for j in range(1, PACK - 1):
             nc.sync.dma_start(planes[j][:], x_rows[:, j, :])
-        for c in range(1):
-            load_w(c)
         nc.sync.dma_start(planes[PACK - 1][:], x_rows[:, PACK - 1, :])
-        for c in range(1, len(W_CHUNKS)):
+        for c in range(0, len(W_CHUNKS)):
             load_w(c)
 
         w_grouped = keep.tile([P, PACK, P, PACK], BF16, name="w_grouped", align_bytes=64)
@@ -102,8 +100,8 @@ def tile_picked_andpool_none_lo_kernel(tc, xT, w1, offs, out_0, out_1, out_2):
         rest_grouped = keep.tile([P, HALF, PACK], BF16, name="rest_grouped", tag="w_raw%d" % W_CHUNKS[-1][0], align_bytes=64)
         for d, copy in ((2, nc.scalar.copy), (3, nc.vector.tensor_copy)):
             copy(
-                rest_grouped[:, (d - 2) * V : (d - 1) * V, :].rearrange("p (c i) j -> p c j i", i=4),
-                picked[:, :, d * V : (d + 1) * V].rearrange("p j (c i) -> p c j i", i=4),
+                rest_grouped[:, (d - 2) * V : (d - 1) * V, :],
+                picked[:, :, d * V : (d + 1) * V].rearrange("p j n -> p n j"),
             )
         for d in (2, 3):
             pieces = pieces + quantize_entries(rest_grouped[:, (d - 2) * V : (d - 1) * V, :], d * V, "x_codes%d" % (d * V))

@@ -61,7 +61,8 @@ def tile_picked_andpool_none_lo_kernel(tc, xT, w1, offs, out_0, out_1, out_2):
         nc.scalar.copy(lead_grouped[:, :, 0:2], picked[:, 0:2, :HALF].rearrange("p j n -> p n j"))
         for j in range(2, PACK):
             nc.vector.tensor_copy(lead_grouped[:, :, j], planes[j][:].indirect(offsets[:, : HALF // 16]))
-            nc.vector.tensor_copy(picked[:, j, HALF:], planes[j][:].indirect(offsets[:, HALF // 16 :]))
+            end = S if j < PACK - 1 else S - V
+            nc.vector.tensor_copy(picked[:, j, HALF:end], planes[j][:].indirect(offsets[:, HALF // 16 : end // 16]))
 
         def quantize_entries(grouped, lo, tag):
             width = grouped.shape[1]
@@ -74,7 +75,6 @@ def tile_picked_andpool_none_lo_kernel(tc, xT, w1, offs, out_0, out_1, out_2):
             )
             return [(codes[:, c : c + V], scales[:, c : c + V]) for c in range(0, width, V)]
 
-        pieces = quantize_entries(lead_grouped[:], 0, "x_codes0")
 
         def w_views(c, first, last):
             lo = W_CHUNKS[c][0]
@@ -87,6 +87,7 @@ def tile_picked_andpool_none_lo_kernel(tc, xT, w1, offs, out_0, out_1, out_2):
         c = len(W_CHUNKS) - 1
         nc.scalar.copy(*w_views(c, W_CHUNKS[c][0], P - W_VECTOR))
         nc.vector.tensor_copy(*w_views(c, P - W_VECTOR, P))
+        pieces = quantize_entries(lead_grouped[:], 0, "w_raw0")
 
         w_codes = [keep.tile([P, P], U32, name="w_codes%d" % t, align_bytes=64) for t in range(PACK)]
         w_scales = [keep.tile([P, P], U8, name="w_scales%d" % t, align_bytes=64) for t in range(PACK)]
@@ -98,11 +99,9 @@ def tile_picked_andpool_none_lo_kernel(tc, xT, w1, offs, out_0, out_1, out_2):
             )
 
         rest_grouped = keep.tile([P, HALF, PACK], BF16, name="rest_grouped", tag="w_raw%d" % W_CHUNKS[-1][0], align_bytes=64)
-        for d, copy in ((2, nc.scalar.copy), (3, nc.vector.tensor_copy)):
-            copy(
-                rest_grouped[:, (d - 2) * V : (d - 1) * V, :],
-                picked[:, :, d * V : (d + 1) * V].rearrange("p j n -> p n j"),
-            )
+        nc.scalar.copy(rest_grouped[:, :V, :], picked[:, :, HALF : S - V].rearrange("p j n -> p n j"))
+        nc.vector.tensor_copy(rest_grouped[:, V:, PACK - 1], planes[PACK - 1][:].indirect(offsets[:, (S - V) // 16 :]))
+        nc.vector.tensor_copy(rest_grouped[:, V:, : PACK - 1], picked[:, : PACK - 1, S - V :].rearrange("p j n -> p n j"))
         for d in (2, 3):
             pieces = pieces + quantize_entries(rest_grouped[:, (d - 2) * V : (d - 1) * V, :], d * V, "x_codes%d" % (d * V))
 

@@ -19,7 +19,6 @@ SIGMOID = mybir.ActivationFunctionType.Sigmoid
 MULT = mybir.AluOpType.mult
 COLS = V // 16
 W_CHUNKS = ((0, 64), (64, 128))
-W_VECTOR = 50
 
 
 def tile_picked_andpool_none_lo_kernel(tc, xT, w1, offs, out_0, out_1, out_2):
@@ -55,14 +54,12 @@ def tile_picked_andpool_none_lo_kernel(tc, xT, w1, offs, out_0, out_1, out_2):
         w_grouped = keep.tile([P, PACK, P, PACK], BF16, name="w_grouped", align_bytes=64)
         picked = keep.tile([P, PACK, S], BF16, name="picked", align_bytes=64)
         HALF = S // 2
-        lead_grouped = keep.tile([P, HALF, PACK], BF16, name="lead_grouped", align_bytes=64)
-        for j in range(2):
+        grouped = keep.tile([P, S, PACK], BF16, name="grouped", align_bytes=64)
+        for j in range(PACK):
             nc.vector.tensor_copy(picked[:, j, :], planes[j][:].indirect(offsets[:]))
-        nc.scalar.copy(lead_grouped[:, :, 0:2], picked[:, 0:2, :HALF].rearrange("p j n -> p n j"))
-        for j in range(2, PACK):
-            nc.vector.tensor_copy(lead_grouped[:, :, j], planes[j][:].indirect(offsets[:, : HALF // 16]))
-            end = S if j < PACK - 1 else S - V
-            nc.vector.tensor_copy(picked[:, j, HALF:end], planes[j][:].indirect(offsets[:, HALF // 16 : end // 16]))
+        nc.scalar.copy(grouped[:, :, 0:2], picked[:, 0:2, :].rearrange("p j n -> p n j"))
+        for lo in (0, HALF):
+            nc.vector.tensor_copy(grouped[:, lo : lo + HALF, 2:4], picked[:, 2:4, lo : lo + HALF].rearrange("p j n -> p n j"))
 
         def quantize_entries(grouped, lo, tag):
             width = grouped.shape[1]
@@ -73,21 +70,21 @@ def tile_picked_andpool_none_lo_kernel(tc, xT, w1, offs, out_0, out_1, out_2):
                 scales=scales[:],
                 in_=grouped.rearrange("p n j -> p (n j)"),
             )
-            return [(codes[:, c : c + V], scales[:, c : c + V]) for c in range(0, width, V)]
+            return codes, scales
 
+        lead_codes, lead_scales = quantize_entries(grouped[:, :HALF, :], 0, "lead_codes")
+        lead = (lead_codes[:], lead_scales[:])
 
-        def w_views(c, first, last):
+        def w_views(c, first, last, t0, t1):
             lo = W_CHUNKS[c][0]
-            dst = w_grouped[:, :, first:last, :].rearrange("p t m j -> p m t j")
-            src = w_raw[c][:].rearrange("p j (m t) -> p m t j", t=PACK)[:, first - lo : last - lo, :, :]
+            dst = w_grouped[:, t0:t1, first:last, :].rearrange("p t m j -> p m t j")
+            src = w_raw[c][:].rearrange("p j (m t) -> p m t j", t=PACK)[:, first - lo : last - lo, t0:t1, :]
             return dst, src
 
-        for c, (lo, hi) in enumerate(W_CHUNKS[:-1]):
-            nc.scalar.copy(*w_views(c, lo, hi))
-        c = len(W_CHUNKS) - 1
-        nc.scalar.copy(*w_views(c, W_CHUNKS[c][0], P - W_VECTOR))
-        nc.vector.tensor_copy(*w_views(c, P - W_VECTOR, P))
-        pieces = quantize_entries(lead_grouped[:], 0, "w_raw0")
+        nc.scalar.copy(*w_views(0, 0, 64, 0, PACK))
+        nc.vector.tensor_copy(*w_views(1, 64, P, 0, 1))
+        nc.vector.tensor_copy(*w_views(1, 64, P, 1, 2))
+        nc.scalar.copy(*w_views(1, 64, P, 2, PACK))
 
         w_codes = [keep.tile([P, P], U32, name="w_codes%d" % t, align_bytes=64) for t in range(PACK)]
         w_scales = [keep.tile([P, P], U8, name="w_scales%d" % t, align_bytes=64) for t in range(PACK)]
@@ -98,39 +95,44 @@ def tile_picked_andpool_none_lo_kernel(tc, xT, w1, offs, out_0, out_1, out_2):
                 in_=w_grouped[:, t, :, :].rearrange("p m j -> p (m j)"),
             )
 
-        rest_grouped = keep.tile([P, HALF, PACK], BF16, name="rest_grouped", tag="w_raw%d" % W_CHUNKS[-1][0], align_bytes=64)
-        nc.scalar.copy(rest_grouped[:, :V, :], picked[:, :, HALF : S - V].rearrange("p j n -> p n j"))
-        nc.vector.tensor_copy(rest_grouped[:, V:, PACK - 1], planes[PACK - 1][:].indirect(offsets[:, (S - V) // 16 :]))
-        nc.vector.tensor_copy(rest_grouped[:, V:, : PACK - 1], picked[:, : PACK - 1, S - V :].rearrange("p j n -> p n j"))
-        for d in (2, 3):
-            pieces = pieces + quantize_entries(rest_grouped[:, (d - 2) * V : (d - 1) * V, :], d * V, "x_codes%d" % (d * V))
+        rest_codes, rest_scales = quantize_entries(grouped[:, HALF:, :], HALF, "w_raw64")
+        rest = {d: (rest_codes[:, (d - 2) * V : (d - 1) * V], rest_scales[:, (d - 2) * V : (d - 1) * V]) for d in (2, 3)}
+
+        def multiply(out, t, entries):
+            codes, scales = entries
+            nc.tensor.matmul_mx(
+                out=out,
+                lhsT=w_codes[t][:].bitcast(FP8X4),
+                lhsT_scale=w_scales[t][:],
+                rhs=codes.bitcast(FP8X4),
+                rhs_scale=scales,
+                start=True,
+                stop=True,
+            )
+
+        def lead_product(u):
+            truth = keep.tile([P, 2, 2, V], F32, name="lead_truth%d" % u)
+            for e in range(2):
+                bank = psum.tile([P, 2 * V], F32, name="lead_bank%d%d" % (u, e))
+                multiply(bank[:], 2 * u + e, lead)
+                nc.scalar.activation(truth[:, e, :, :].rearrange("p d v -> p (d v)"), bank[:], SIGMOID)
+            product = keep.tile([P, 2, V], F32, name="lead_product%d" % u)
+            nc.vector.tensor_tensor(product[:], truth[:, :, 0, :], truth[:, :, 1, :], MULT)
+            return product
 
         def truth_values(u, d):
-            codes, scales = pieces[d]
             bank = psum.tile([P, 2, V], F32, name="bank%d%d" % (u, d))
             for e in range(2):
-                t = 2 * u + e
-                nc.tensor.matmul_mx(
-                    out=bank[:, e, :],
-                    lhsT=w_codes[t][:].bitcast(FP8X4),
-                    lhsT_scale=w_scales[t][:],
-                    rhs=codes.bitcast(FP8X4),
-                    rhs_scale=scales,
-                    start=True,
-                    stop=True,
-                )
+                multiply(bank[:, e, :], 2 * u + e, rest[d])
             truth = keep.tile([P, 2, V], F32, name="truth%d%d" % (u, d))
             nc.scalar.activation(truth[:], bank[:], SIGMOID)
             return truth
 
         y_grouped = keep.tile([P, V, PACK], BF16, name="y_grouped", align_bytes=64)
         out_rows = out_0.rearrange("(p t) v -> p t v", t=PACK)
-        running = {}
-        for u, d in ((0, 0), (0, 1), (1, 0), (1, 1), (0, 2), (1, 2), (0, 3), (1, 3)):
+        running = {u: lead_product(u) for u in range(2)}
+        for u, d in ((0, 2), (1, 2), (0, 3), (1, 3)):
             truth = truth_values(u, d)
-            if d == 0:
-                running[u] = truth
-                continue
             if (u, d) == (1, D - 1):
                 nc.vector.tensor_tensor(
                     y_grouped[:, :, 2:4],

@@ -55,11 +55,20 @@ def tile_picked_andpool_none_lo_kernel(tc, xT, w1, offs, out_0, out_1, out_2):
         picked = keep.tile([P, PACK, S], BF16, name="picked", align_bytes=64)
         HALF = S // 2
         grouped = keep.tile([P, S, PACK], BF16, name="grouped", align_bytes=64)
-        for j in range(PACK):
-            nc.vector.tensor_copy(picked[:, j, :], planes[j][:].indirect(offsets[:]))
+        def gather(j, lo, hi):
+            nc.vector.tensor_copy(picked[:, j, lo:hi], planes[j][:].indirect(offsets[:, lo // 16 : hi // 16]))
+
+        def weave_upper(lo, hi):
+            nc.vector.tensor_copy(grouped[:, lo:hi, 2:4], picked[:, 2:4, lo:hi].rearrange("p j n -> p n j"))
+
+        rounded = keep.tile([P, T], BF16, name="rounded", align_bytes=64)
+        nc.vector.tensor_copy(rounded[:], planes[0][:])
+        nc.scalar.activation(picked[:, 0, :], rounded[:].indirect(offsets[:]), mybir.ActivationFunctionType.Copy)
+        for j in range(1, PACK - 1):
+            gather(j, 0, S)
         nc.scalar.copy(grouped[:, :, 0:2], picked[:, 0:2, :].rearrange("p j n -> p n j"))
-        for lo in (0, HALF):
-            nc.vector.tensor_copy(grouped[:, lo : lo + HALF, 2:4], picked[:, 2:4, lo : lo + HALF].rearrange("p j n -> p n j"))
+        gather(PACK - 1, 0, HALF)
+        weave_upper(0, HALF)
 
         def quantize_entries(grouped, lo, tag):
             width = grouped.shape[1]
@@ -74,6 +83,8 @@ def tile_picked_andpool_none_lo_kernel(tc, xT, w1, offs, out_0, out_1, out_2):
 
         lead_codes, lead_scales = quantize_entries(grouped[:, :HALF, :], 0, "lead_codes")
         lead = (lead_codes[:], lead_scales[:])
+        gather(PACK - 1, HALF, S)
+        weave_upper(HALF, S)
 
         def w_views(c, first, last, t0, t1):
             lo = W_CHUNKS[c][0]
@@ -81,7 +92,8 @@ def tile_picked_andpool_none_lo_kernel(tc, xT, w1, offs, out_0, out_1, out_2):
             src = w_raw[c][:].rearrange("p j (m t) -> p m t j", t=PACK)[:, first - lo : last - lo, t0:t1, :]
             return dst, src
 
-        nc.scalar.copy(*w_views(0, 0, 64, 0, PACK))
+        nc.scalar.copy(*w_views(0, 0, 64, 0, 2))
+        nc.scalar.copy(*w_views(0, 0, 64, 2, PACK))
         nc.vector.tensor_copy(*w_views(1, 64, P, 0, 1))
         nc.vector.tensor_copy(*w_views(1, 64, P, 1, 2))
         nc.scalar.copy(*w_views(1, 64, P, 2, PACK))
@@ -141,11 +153,18 @@ def tile_picked_andpool_none_lo_kernel(tc, xT, w1, offs, out_0, out_1, out_2):
                     MULT,
                 )
             product = keep.tile([P, 2, V], F32, name="product%d%d" % (u, d))
-            nc.vector.tensor_tensor(product[:], running[u][:], truth[:], MULT)
+            if (u, d) == (0, D - 1):
+                for lo in (0, V // 2):
+                    part = slice(lo, lo + V // 2)
+                    nc.vector.tensor_tensor(product[:, :, part], running[u][:, :, part], truth[:, :, part], MULT)
+            else:
+                nc.vector.tensor_tensor(product[:], running[u][:], truth[:], MULT)
             running[u] = product
         for u in range(2):
             nc.sync.dma_start(out_rows[:, 2 * u : 2 * u + 2, :], running[u][:])
-        nc.scalar.copy(y_grouped[:, :, 0:2], running[0][:].rearrange("p t v -> p v t"))
+        for lo in (0, V // 2):
+            part = slice(lo, lo + V // 2)
+            nc.scalar.copy(y_grouped[:, part, 0:2], running[0][:, :, part].rearrange("p t v -> p v t"))
 
         y_codes = keep.tile([P, V], U32, name="y_codes", align_bytes=64)
         y_scales = keep.tile([P, V], U8, name="y_scales", align_bytes=64)

@@ -18,6 +18,7 @@ FP8X4 = mybir.dt.float8_e4m3fn_x4
 SIGMOID = mybir.ActivationFunctionType.Sigmoid
 MULT = mybir.AluOpType.mult
 COLS = V // 16
+W_VECTOR = 16
 W_CHUNKS = ((0, 64), (64, 128))
 
 
@@ -92,11 +93,11 @@ def tile_picked_andpool_none_lo_kernel(tc, xT, w1, offs, out_0, out_1, out_2):
             src = w_raw[c][:].rearrange("p j (m t) -> p m t j", t=PACK)[:, first - lo : last - lo, t0:t1, :]
             return dst, src
 
-        nc.scalar.copy(*w_views(0, 0, 64, 0, 2))
-        nc.scalar.copy(*w_views(0, 0, 64, 2, PACK))
+        nc.scalar.copy(*w_views(0, 0, 64 - W_VECTOR, 0, PACK))
+        nc.vector.tensor_copy(*w_views(0, 64 - W_VECTOR, 64, 0, PACK))
         nc.vector.tensor_copy(*w_views(1, 64, P, 0, 1))
-        nc.vector.tensor_copy(*w_views(1, 64, P, 1, 2))
-        nc.scalar.copy(*w_views(1, 64, P, 2, PACK))
+        nc.vector.tensor_copy(*w_views(1, 64, 96, 1, PACK))
+        nc.scalar.copy(*w_views(1, 96, P, 1, PACK))
 
         w_codes = [keep.tile([P, P], U32, name="w_codes%d" % t, align_bytes=64) for t in range(PACK)]
         w_scales = [keep.tile([P, P], U8, name="w_scales%d" % t, align_bytes=64) for t in range(PACK)]

@@ -3,7 +3,6 @@ from contextlib import ExitStack
 import concourse.mybir as mybir
 
 K, T, S, V, N = 512, 1024, 512, 128, 512
-D = S // V
 P = 128
 PACK = 4
 FLOPS = 2 * K * N * S
@@ -17,9 +16,11 @@ U8 = mybir.dt.uint8
 FP8X4 = mybir.dt.float8_e4m3fn_x4
 SIGMOID = mybir.ActivationFunctionType.Sigmoid
 MULT = mybir.AluOpType.mult
-COLS = V // 16
-W_VECTOR = 16
-W_CHUNKS = ((0, 64), (64, 128))
+
+ENTRIES_A_COLUMN = 16
+LEAD = 2 * V
+W_HALF = P // 2
+W_VECTOR = 36
 
 
 def tile_picked_andpool_none_lo_kernel(tc, xT, w1, offs, out_0, out_1, out_2):
@@ -35,84 +36,71 @@ def tile_picked_andpool_none_lo_kernel(tc, xT, w1, offs, out_0, out_1, out_2):
 
         x_rows = xT.rearrange("(p j) t -> p j t", j=PACK)
         w_rows = w1.rearrange("(p j) c -> p j c", j=PACK)
-        offsets = keep.tile([P, S // 16], U16, name="offsets")
+        offsets = keep.tile([P, S // ENTRIES_A_COLUMN], U16, name="offsets")
         planes = [keep.tile([P, T], F32, name="plane%d" % j) for j in range(PACK)]
-        w_raw = [keep.tile([P, PACK, PACK * (hi - lo)], F32, name="w_raw%d" % lo, tag="w_raw%d" % lo, align_bytes=64) for lo, hi in W_CHUNKS]
+        w_raw = [keep.tile([P, PACK, N // 2], F32, name="w_raw%d" % h, tag="w_raw%d" % h, align_bytes=64) for h in range(2)]
 
         nc.sync.dma_start(planes[0][:], x_rows[:, 0, :])
         nc.sync.dma_start(offsets[:], offs)
-
-        def load_w(c):
-            lo, hi = W_CHUNKS[c]
-            nc.sync.dma_start(w_raw[c][:], w_rows[:, :, PACK * lo : PACK * hi])
-
-        for j in range(1, PACK - 1):
+        for j in range(1, PACK):
             nc.sync.dma_start(planes[j][:], x_rows[:, j, :])
-        nc.sync.dma_start(planes[PACK - 1][:], x_rows[:, PACK - 1, :])
-        for c in range(0, len(W_CHUNKS)):
-            load_w(c)
+        for h in range(2):
+            nc.sync.dma_start(w_raw[h][:], w_rows[:, :, h * (N // 2) : (h + 1) * (N // 2)])
 
         w_grouped = keep.tile([P, PACK, P, PACK], BF16, name="w_grouped", align_bytes=64)
         picked = keep.tile([P, PACK, S], BF16, name="picked", align_bytes=64)
-        HALF = S // 2
-        grouped = keep.tile([P, S, PACK], BF16, name="grouped", align_bytes=64)
+        x_grouped = keep.tile([P, S, PACK], BF16, name="x_grouped", align_bytes=64)
+
         def gather(j, lo, hi):
-            nc.vector.tensor_copy(picked[:, j, lo:hi], planes[j][:].indirect(offsets[:, lo // 16 : hi // 16]))
+            columns = offsets[:, lo // ENTRIES_A_COLUMN : hi // ENTRIES_A_COLUMN]
+            nc.vector.tensor_copy(picked[:, j, lo:hi], planes[j][:].indirect(columns))
 
-        def weave_upper(lo, hi):
-            nc.vector.tensor_copy(grouped[:, lo:hi, 2:4], picked[:, 2:4, lo:hi].rearrange("p j n -> p n j"))
+        def weave(copy, into, first_plane, last_plane, lo, hi):
+            copy(into, picked[:, first_plane:last_plane, lo:hi].rearrange("p j n -> p n j"))
 
-        rounded = keep.tile([P, T], BF16, name="rounded", align_bytes=64)
-        nc.vector.tensor_copy(rounded[:], planes[0][:])
-        nc.scalar.activation(picked[:, 0, :], rounded[:].indirect(offsets[:]), mybir.ActivationFunctionType.Copy)
-        for j in range(1, PACK - 1):
+        def quantize(codes, scales, grouped):
+            nc.vector.quantize_mx(out=codes.bitcast(FP8X4), scales=scales, in_=grouped.rearrange("p n j -> p (n j)"))
+
+        for j in range(PACK - 1):
             gather(j, 0, S)
-        nc.scalar.copy(grouped[:, :, 0:2], picked[:, 0:2, :].rearrange("p j n -> p n j"))
-        gather(PACK - 1, 0, HALF)
-        weave_upper(0, HALF)
+        for lo, hi in ((0, LEAD), (S - V, S)):
+            weave(nc.scalar.copy, x_grouped[:, lo:hi, 0:2], 0, 2, lo, hi)
+        gather(PACK - 1, 0, LEAD)
+        for lo in (0, V):
+            weave(nc.vector.tensor_copy, x_grouped[:, lo : lo + V, 2:4], 2, 4, lo, lo + V)
 
-        def quantize_entries(grouped, lo, tag):
-            width = grouped.shape[1]
-            codes = keep.tile([P, width], U32, name="x_codes%d" % lo, tag=tag, align_bytes=64)
-            scales = keep.tile([P, width], U8, name="x_scales%d" % lo, align_bytes=64)
-            nc.vector.quantize_mx(
-                out=codes[:].bitcast(FP8X4),
-                scales=scales[:],
-                in_=grouped.rearrange("p n j -> p (n j)"),
-            )
-            return codes, scales
+        lead_codes = keep.tile([P, LEAD], U32, name="lead_codes", align_bytes=64)
+        lead_scales = keep.tile([P, LEAD], U8, name="lead_scales", align_bytes=64)
+        for lo in (0, V):
+            quantize(lead_codes[:, lo : lo + V], lead_scales[:, lo : lo + V], x_grouped[:, lo : lo + V, :])
+        gather(PACK - 1, LEAD, S)
+        weave(nc.vector.tensor_copy, x_grouped[:, S - V :, 2:4], 2, 4, S - V, S)
 
-        lead_codes, lead_scales = quantize_entries(grouped[:, :HALF, :], 0, "lead_codes")
-        lead = (lead_codes[:], lead_scales[:])
-        gather(PACK - 1, HALF, S)
-        weave_upper(HALF, S)
-
-        def w_views(c, first, last, t0, t1):
-            lo = W_CHUNKS[c][0]
-            dst = w_grouped[:, t0:t1, first:last, :].rearrange("p t m j -> p m t j")
-            src = w_raw[c][:].rearrange("p j (m t) -> p m t j", t=PACK)[:, first - lo : last - lo, t0:t1, :]
+        def w_views(h, first, last, first_t, last_t):
+            dst = w_grouped[:, first_t:last_t, h * W_HALF + first : h * W_HALF + last, :].rearrange("p t m j -> p m t j")
+            src = w_raw[h][:].rearrange("p j (m t) -> p m t j", t=PACK)[:, first:last, first_t:last_t, :]
             return dst, src
 
-        nc.scalar.copy(*w_views(0, 0, 64 - W_VECTOR, 0, PACK))
-        nc.vector.tensor_copy(*w_views(0, 64 - W_VECTOR, 64, 0, PACK))
-        nc.vector.tensor_copy(*w_views(1, 64, P, 0, 1))
-        nc.vector.tensor_copy(*w_views(1, 64, 96, 1, PACK))
-        nc.scalar.copy(*w_views(1, 96, P, 1, PACK))
+        nc.scalar.copy(*w_views(0, 0, W_HALF, 0, PACK))
+        nc.vector.tensor_copy(*w_views(1, 0, W_HALF, 0, 1))
+        nc.vector.tensor_copy(*w_views(1, 0, W_VECTOR, 1, PACK))
+        nc.scalar.copy(*w_views(1, W_VECTOR, W_HALF, 1, PACK))
 
         w_codes = [keep.tile([P, P], U32, name="w_codes%d" % t, align_bytes=64) for t in range(PACK)]
         w_scales = [keep.tile([P, P], U8, name="w_scales%d" % t, align_bytes=64) for t in range(PACK)]
         for t in range(PACK):
-            nc.vector.quantize_mx(
-                out=w_codes[t][:].bitcast(FP8X4),
-                scales=w_scales[t][:],
-                in_=w_grouped[:, t, :, :].rearrange("p m j -> p (m j)"),
-            )
+            quantize(w_codes[t][:], w_scales[t][:], w_grouped[:, t, :, :])
 
-        rest_codes, rest_scales = quantize_entries(grouped[:, HALF:, :], HALF, "w_raw64")
-        rest = {d: (rest_codes[:, (d - 2) * V : (d - 1) * V], rest_scales[:, (d - 2) * V : (d - 1) * V]) for d in (2, 3)}
+        piece2_grouped = keep.tile([P, V, PACK], BF16, name="piece2_grouped", tag="w_raw1", align_bytes=64)
+        weave(nc.scalar.copy, piece2_grouped[:], 0, PACK, LEAD, S - V)
+        late = {}
+        for d, grouped, tag in ((2, piece2_grouped[:], "piece2_codes"), (3, x_grouped[:, S - V :, :], "w_raw1")):
+            codes = keep.tile([P, V], U32, name="piece%d_codes" % d, tag=tag, align_bytes=64)
+            scales = keep.tile([P, V], U8, name="piece%d_scales" % d, align_bytes=64)
+            quantize(codes[:], scales[:], grouped)
+            late[d] = (codes[:], scales[:])
 
-        def multiply(out, t, entries):
-            codes, scales = entries
+        def multiply(out, t, codes, scales):
             nc.tensor.matmul_mx(
                 out=out,
                 lhsT=w_codes[t][:].bitcast(FP8X4),
@@ -126,8 +114,8 @@ def tile_picked_andpool_none_lo_kernel(tc, xT, w1, offs, out_0, out_1, out_2):
         def lead_product(u):
             truth = keep.tile([P, 2, 2, V], F32, name="lead_truth%d" % u)
             for e in range(2):
-                bank = psum.tile([P, 2 * V], F32, name="lead_bank%d%d" % (u, e))
-                multiply(bank[:], 2 * u + e, lead)
+                bank = psum.tile([P, LEAD], F32, name="lead_bank%d%d" % (u, e))
+                multiply(bank[:], 2 * u + e, lead_codes[:], lead_scales[:])
                 nc.scalar.activation(truth[:, e, :, :].rearrange("p d v -> p (d v)"), bank[:], SIGMOID)
             product = keep.tile([P, 2, V], F32, name="lead_product%d" % u)
             nc.vector.tensor_tensor(product[:], truth[:, :, 0, :], truth[:, :, 1, :], MULT)
@@ -136,44 +124,45 @@ def tile_picked_andpool_none_lo_kernel(tc, xT, w1, offs, out_0, out_1, out_2):
         def truth_values(u, d):
             bank = psum.tile([P, 2, V], F32, name="bank%d%d" % (u, d))
             for e in range(2):
-                multiply(bank[:, e, :], 2 * u + e, rest[d])
+                multiply(bank[:, e, :], 2 * u + e, *late[d])
             truth = keep.tile([P, 2, V], F32, name="truth%d%d" % (u, d))
             nc.scalar.activation(truth[:], bank[:], SIGMOID)
             return truth
 
         y_grouped = keep.tile([P, V, PACK], BF16, name="y_grouped", align_bytes=64)
-        out_rows = out_0.rearrange("(p t) v -> p t v", t=PACK)
-        running = {u: lead_product(u) for u in range(2)}
-        for u, d in ((0, 2), (1, 2), (0, 3), (1, 3)):
-            truth = truth_values(u, d)
-            if (u, d) == (1, D - 1):
-                nc.vector.tensor_tensor(
-                    y_grouped[:, :, 2:4],
-                    running[u][:].rearrange("p t v -> p v t"),
-                    truth[:].rearrange("p t v -> p v t"),
-                    MULT,
-                )
-            product = keep.tile([P, 2, V], F32, name="product%d%d" % (u, d))
-            if (u, d) == (0, D - 1):
-                for lo in (0, V // 2):
-                    part = slice(lo, lo + V // 2)
-                    nc.vector.tensor_tensor(product[:, :, part], running[u][:, :, part], truth[:, :, part], MULT)
-            else:
-                nc.vector.tensor_tensor(product[:], running[u][:], truth[:], MULT)
-            running[u] = product
+        two_pieces = [lead_product(u) for u in range(2)]
+        three_pieces = []
         for u in range(2):
-            nc.sync.dma_start(out_rows[:, 2 * u : 2 * u + 2, :], running[u][:])
-        for lo in (0, V // 2):
-            part = slice(lo, lo + V // 2)
-            nc.scalar.copy(y_grouped[:, part, 0:2], running[0][:, :, part].rearrange("p t v -> p v t"))
+            truth = truth_values(u, 2)
+            product = keep.tile([P, 2, V], F32, name="three_pieces%d" % u)
+            nc.vector.tensor_tensor(product[:], two_pieces[u][:], truth[:], MULT)
+            three_pieces.append(product)
+
+        v_halves = (slice(0, V // 2), slice(V // 2, V))
+        truth = truth_values(0, 3)
+        result0 = keep.tile([P, 2, V], F32, name="result0")
+        for part in v_halves:
+            nc.vector.tensor_tensor(result0[:, :, part], three_pieces[0][:, :, part], truth[:, :, part], MULT)
+
+        truth = truth_values(1, 3)
+        nc.vector.tensor_tensor(
+            y_grouped[:, :, 2:4],
+            three_pieces[1][:].rearrange("p e v -> p v e"),
+            truth[:].rearrange("p e v -> p v e"),
+            MULT,
+        )
+        result1 = keep.tile([P, 2, V], F32, name="result1")
+        nc.vector.tensor_tensor(result1[:], three_pieces[1][:], truth[:], MULT)
+
+        out_rows = out_0.rearrange("(p t) v -> p t v", t=PACK)
+        for u, result in enumerate((result0, result1)):
+            nc.sync.dma_start(out_rows[:, 2 * u : 2 * u + 2, :], result[:])
+        for part in v_halves:
+            nc.scalar.copy(y_grouped[:, part, 0:2], result0[:, :, part].rearrange("p e v -> p v e"))
 
         y_codes = keep.tile([P, V], U32, name="y_codes", align_bytes=64)
         y_scales = keep.tile([P, V], U8, name="y_scales", align_bytes=64)
-        nc.vector.quantize_mx(
-            out=y_codes[:].bitcast(FP8X4),
-            scales=y_scales[:],
-            in_=y_grouped[:].rearrange("p v t -> p (v t)"),
-        )
+        quantize(y_codes[:], y_scales[:], y_grouped[:])
         nc.sync.dma_start(out_1.rearrange("z l c r -> (z l) (c r)").bitcast(I32), y_codes[:].bitcast(I32))
         scale_rows = out_2.rearrange("z q c -> (z q) c").bitcast(I32)
         for q in range(4):

@@ -20,13 +20,14 @@ MULT = mybir.AluOpType.mult
 ENTRIES_A_COLUMN = 16
 LEAD = 2 * V
 W_HALF = P // 2
-W_VECTOR = 36
+W_VECTOR = 0
 
 
 def tile_picked_andpool_none_lo_kernel(tc, xT, w1, offs, out_0, out_1, out_2):
     nc = tc.nc
     with ExitStack() as ctx:
         keep = ctx.enter_context(tc.tile_pool(name="keep", bufs=1))
+        shared = ctx.enter_context(tc.tile_pool(name="shared", bufs=1))
         psum = ctx.enter_context(tc.psum_pool(name="psum", bufs=1))
 
         warm_in = keep.tile([P, 1], F32, name="warm_in")
@@ -38,7 +39,10 @@ def tile_picked_andpool_none_lo_kernel(tc, xT, w1, offs, out_0, out_1, out_2):
         w_rows = w1.rearrange("(p j) c -> p j c", j=PACK)
         offsets = keep.tile([P, S // ENTRIES_A_COLUMN], U16, name="offsets")
         planes = [keep.tile([P, T], F32, name="plane%d" % j) for j in range(PACK)]
-        w_raw = [keep.tile([P, PACK, N // 2], F32, name="w_raw%d" % h, tag="w_raw%d" % h, align_bytes=64) for h in range(2)]
+        w_raw = [
+            shared.tile([P, PACK, N // 2], F32, name="w_raw0", align_bytes=64, offset=0),
+            keep.tile([P, PACK, N // 2], F32, name="w_raw1", tag="w_raw1", align_bytes=64),
+        ]
 
         nc.sync.dma_start(planes[0][:], x_rows[:, 0, :])
         nc.sync.dma_start(offsets[:], offs)
@@ -49,7 +53,7 @@ def tile_picked_andpool_none_lo_kernel(tc, xT, w1, offs, out_0, out_1, out_2):
 
         w_grouped = keep.tile([P, PACK, P, PACK], BF16, name="w_grouped", align_bytes=64)
         picked = keep.tile([P, PACK, S], BF16, name="picked", align_bytes=64)
-        x_grouped = keep.tile([P, S, PACK], BF16, name="x_grouped", align_bytes=64)
+        x_grouped = keep.tile([P, S - V, PACK], BF16, name="x_grouped", align_bytes=64)
 
         def gather(j, lo, hi):
             columns = offsets[:, lo // ENTRIES_A_COLUMN : hi // ENTRIES_A_COLUMN]
@@ -63,42 +67,41 @@ def tile_picked_andpool_none_lo_kernel(tc, xT, w1, offs, out_0, out_1, out_2):
 
         for j in range(PACK - 1):
             gather(j, 0, S)
-        for lo, hi in ((0, LEAD), (S - V, S)):
-            weave(nc.scalar.copy, x_grouped[:, lo:hi, 0:2], 0, 2, lo, hi)
-        gather(PACK - 1, 0, LEAD)
-        for lo in (0, V):
-            weave(nc.vector.tensor_copy, x_grouped[:, lo : lo + V, 2:4], 2, 4, lo, lo + V)
+        weave(nc.scalar.copy, x_grouped[:, :, 0:2], 0, 2, 0, S - V)
+        gather(PACK - 1, 0, S - V)
+        gather(PACK - 1, S - V, S)
+        weave(nc.vector.tensor_copy, x_grouped[:, :, 2:4], 2, 4, 0, S - V)
 
-        lead_codes = keep.tile([P, LEAD], U32, name="lead_codes", align_bytes=64)
-        lead_scales = keep.tile([P, LEAD], U8, name="lead_scales", align_bytes=64)
-        for lo in (0, V):
-            quantize(lead_codes[:, lo : lo + V], lead_scales[:, lo : lo + V], x_grouped[:, lo : lo + V, :])
-        gather(PACK - 1, LEAD, S)
-        weave(nc.vector.tensor_copy, x_grouped[:, S - V :, 2:4], 2, 4, S - V, S)
 
         def w_views(h, first, last, first_t, last_t):
-            dst = w_grouped[:, first_t:last_t, h * W_HALF + first : h * W_HALF + last, :].rearrange("p t m j -> p m t j")
-            src = w_raw[h][:].rearrange("p j (m t) -> p m t j", t=PACK)[:, first:last, first_t:last_t, :]
+            dst = w_grouped[:, first_t:last_t, h * W_HALF + first : h * W_HALF + last, :].rearrange("p t m j -> p m j t")
+            src = w_raw[h][:].rearrange("p j (m t) -> p m j t", t=PACK)[:, first:last, :, first_t:last_t]
             return dst, src
 
         nc.scalar.copy(*w_views(0, 0, W_HALF, 0, PACK))
-        nc.vector.tensor_copy(*w_views(1, 0, W_HALF, 0, 1))
-        nc.vector.tensor_copy(*w_views(1, 0, W_VECTOR, 1, PACK))
-        nc.scalar.copy(*w_views(1, W_VECTOR, W_HALF, 1, PACK))
+        nc.vector.tensor_copy(*w_views(1, 0, W_HALF, 0, 2))
+        nc.scalar.copy(*w_views(1, 0, W_HALF, 2, PACK))
+
+        lead_codes = shared.tile([P, LEAD], U32, name="lead_codes", align_bytes=64, offset=0)
+        lead_scales = keep.tile([P, LEAD], U8, name="lead_scales", align_bytes=64)
+        quantize(lead_codes[:], lead_scales[:], x_grouped[:, :LEAD, :])
 
         w_codes = [keep.tile([P, P], U32, name="w_codes%d" % t, align_bytes=64) for t in range(PACK)]
         w_scales = [keep.tile([P, P], U8, name="w_scales%d" % t, align_bytes=64) for t in range(PACK)]
         for t in range(PACK):
             quantize(w_codes[t][:], w_scales[t][:], w_grouped[:, t, :, :])
 
-        piece2_grouped = keep.tile([P, V, PACK], BF16, name="piece2_grouped", tag="w_raw1", align_bytes=64)
-        weave(nc.scalar.copy, piece2_grouped[:], 0, PACK, LEAD, S - V)
+        piece3_grouped = keep.tile([P, V, PACK], BF16, name="piece3_grouped", tag="w_raw1", align_bytes=64)
+        nc.scalar.copy(piece3_grouped[:].rearrange("p (c i) j -> p c j i", i=4), picked[:, :, S - V :].rearrange("p j (c i) -> p c j i", i=4))
+        late_codes = (
+            shared.tile([P, V], U32, name="piece2_codes", align_bytes=64, offset=4 * LEAD),
+            keep.tile([P, V], U32, name="piece3_codes", align_bytes=64),
+        )
         late = {}
-        for d, grouped, tag in ((2, piece2_grouped[:], "piece2_codes"), (3, x_grouped[:, S - V :, :], "w_raw1")):
-            codes = keep.tile([P, V], U32, name="piece%d_codes" % d, tag=tag, align_bytes=64)
+        for d, grouped in ((2, x_grouped[:, LEAD:, :]), (3, piece3_grouped[:])):
             scales = keep.tile([P, V], U8, name="piece%d_scales" % d, align_bytes=64)
-            quantize(codes[:], scales[:], grouped)
-            late[d] = (codes[:], scales[:])
+            quantize(late_codes[d - 2][:], scales[:], grouped)
+            late[d] = (late_codes[d - 2][:], scales[:])
 
         def multiply(out, t, codes, scales):
             nc.tensor.matmul_mx(

@@ -53,7 +53,7 @@ def tile_picked_andpool_none_lo_kernel(tc, xT, w1, offs, out_0, out_1, out_2):
 
         w_grouped = keep.tile([P, PACK, P, PACK], BF16, name="w_grouped", align_bytes=64)
         picked = keep.tile([P, PACK, S], BF16, name="picked", align_bytes=64)
-        x_grouped = keep.tile([P, S - V, PACK], BF16, name="x_grouped", align_bytes=64)
+        x_grouped = keep.tile([P, LEAD, PACK], BF16, name="x_grouped", align_bytes=64)
 
         def gather(j, lo, hi):
             columns = offsets[:, lo // ENTRIES_A_COLUMN : hi // ENTRIES_A_COLUMN]
@@ -67,10 +67,10 @@ def tile_picked_andpool_none_lo_kernel(tc, xT, w1, offs, out_0, out_1, out_2):
 
         for j in range(PACK - 1):
             gather(j, 0, S)
-        weave(nc.scalar.copy, x_grouped[:, :, 0:2], 0, 2, 0, S - V)
-        gather(PACK - 1, 0, S - V)
-        gather(PACK - 1, S - V, S)
-        weave(nc.vector.tensor_copy, x_grouped[:, :, 2:4], 2, 4, 0, S - V)
+        weave(nc.scalar.copy, x_grouped[:, :, 0:2], 0, 2, 0, LEAD)
+        gather(PACK - 1, 0, LEAD)
+        gather(PACK - 1, LEAD, S)
+        weave(nc.vector.tensor_copy, x_grouped[:, :, 2:4], 2, 4, 0, LEAD)
 
 
         def w_views(h, first, last, first_t, last_t):
@@ -84,24 +84,29 @@ def tile_picked_andpool_none_lo_kernel(tc, xT, w1, offs, out_0, out_1, out_2):
 
         lead_codes = shared.tile([P, LEAD], U32, name="lead_codes", align_bytes=64, offset=0)
         lead_scales = keep.tile([P, LEAD], U8, name="lead_scales", align_bytes=64)
-        quantize(lead_codes[:], lead_scales[:], x_grouped[:, :LEAD, :])
+        quantize(lead_codes[:], lead_scales[:], x_grouped[:])
 
         w_codes = [keep.tile([P, P], U32, name="w_codes%d" % t, align_bytes=64) for t in range(PACK)]
         w_scales = [keep.tile([P, P], U8, name="w_scales%d" % t, align_bytes=64) for t in range(PACK)]
+        late_grouped = (
+            shared.tile([P, V, PACK], BF16, name="piece2_grouped", align_bytes=64, offset=4 * LEAD),
+            keep.tile([P, V, PACK], BF16, name="piece3_grouped", tag="w_raw1", align_bytes=64),
+        )
+        for d in (2, 3):
+            weave(nc.scalar.copy, late_grouped[d - 2][:, :, 0:2], 0, 2, d * V, (d + 1) * V)
         for t in range(PACK):
+            if t == 3:
+                weave(nc.vector.tensor_copy, late_grouped[0][:, :, 2:4], 2, 4, LEAD, S - V)
             quantize(w_codes[t][:], w_scales[t][:], w_grouped[:, t, :, :])
 
-        piece3_grouped = keep.tile([P, V, PACK], BF16, name="piece3_grouped", tag="w_raw1", align_bytes=64)
-        nc.scalar.copy(piece3_grouped[:].rearrange("p (c i) j -> p c j i", i=4), picked[:, :, S - V :].rearrange("p j (c i) -> p c j i", i=4))
-        late_codes = (
-            shared.tile([P, V], U32, name="piece2_codes", align_bytes=64, offset=4 * LEAD),
-            keep.tile([P, V], U32, name="piece3_codes", align_bytes=64),
-        )
         late = {}
-        for d, grouped in ((2, x_grouped[:, LEAD:, :]), (3, piece3_grouped[:])):
+        for d in (2, 3):
+            if d == 3:
+                weave(nc.vector.tensor_copy, late_grouped[1][:, :, 2:4], 2, 4, S - V, S)
+            codes = keep.tile([P, V], U32, name="piece%d_codes" % d, align_bytes=64)
             scales = keep.tile([P, V], U8, name="piece%d_scales" % d, align_bytes=64)
-            quantize(late_codes[d - 2][:], scales[:], grouped)
-            late[d] = (late_codes[d - 2][:], scales[:])
+            quantize(codes[:], scales[:], late_grouped[d - 2][:])
+            late[d] = (codes[:], scales[:])
 
         def multiply(out, t, codes, scales):
             nc.tensor.matmul_mx(

@@ -15,12 +15,13 @@ U16 = mybir.dt.uint16
 U8 = mybir.dt.uint8
 FP8X4 = mybir.dt.float8_e4m3fn_x4
 SIGMOID = mybir.ActivationFunctionType.Sigmoid
+COPY = mybir.ActivationFunctionType.Copy
 MULT = mybir.AluOpType.mult
 
 ENTRIES_A_COLUMN = 16
 LEAD = 2 * V
-W_HALF = P // 2
-W_VECTOR = 0
+W_FIRST = 88
+W_SCALAR = 72
 
 
 def tile_picked_andpool_none_lo_kernel(tc, xT, w1, offs, out_0, out_1, out_2):
@@ -39,9 +40,10 @@ def tile_picked_andpool_none_lo_kernel(tc, xT, w1, offs, out_0, out_1, out_2):
         w_rows = w1.rearrange("(p j) c -> p j c", j=PACK)
         offsets = keep.tile([P, S // ENTRIES_A_COLUMN], U16, name="offsets")
         planes = [keep.tile([P, T], F32, name="plane%d" % j) for j in range(PACK)]
+        w_places = ((0, W_FIRST), (W_FIRST, P))
         w_raw = [
-            shared.tile([P, PACK, N // 2], F32, name="w_raw0", align_bytes=64, offset=0),
-            keep.tile([P, PACK, N // 2], F32, name="w_raw1", tag="w_raw1", align_bytes=64),
+            shared.tile([P, PACK, PACK * W_FIRST], F32, name="w_raw0", align_bytes=64, offset=0),
+            keep.tile([P, PACK, PACK * (P - W_FIRST)], F32, name="w_raw1", align_bytes=64),
         ]
 
         nc.sync.dma_start(planes[0][:], x_rows[:, 0, :])
@@ -49,10 +51,10 @@ def tile_picked_andpool_none_lo_kernel(tc, xT, w1, offs, out_0, out_1, out_2):
         for j in range(1, PACK):
             nc.sync.dma_start(planes[j][:], x_rows[:, j, :])
         for h in range(2):
-            nc.sync.dma_start(w_raw[h][:], w_rows[:, :, h * (N // 2) : (h + 1) * (N // 2)])
+            nc.sync.dma_start(w_raw[h][:], w_rows[:, :, PACK * w_places[h][0] : PACK * w_places[h][1]])
 
         w_grouped = keep.tile([P, PACK, P, PACK], BF16, name="w_grouped", align_bytes=64)
-        picked = keep.tile([P, PACK, S], BF16, name="picked", align_bytes=64)
+        picked = keep.tile([P, PACK, S - V], BF16, name="picked", align_bytes=64)
         x_grouped = keep.tile([P, LEAD, PACK], BF16, name="x_grouped", align_bytes=64)
 
         def gather(j, lo, hi):
@@ -65,48 +67,54 @@ def tile_picked_andpool_none_lo_kernel(tc, xT, w1, offs, out_0, out_1, out_2):
         def quantize(codes, scales, grouped):
             nc.vector.quantize_mx(out=codes.bitcast(FP8X4), scales=scales, in_=grouped.rearrange("p n j -> p (n j)"))
 
+        piece2_grouped = keep.tile([P, V, PACK], BF16, name="piece2_grouped", align_bytes=64)
+        last_piece = offsets[:, (S - V) // ENTRIES_A_COLUMN : S // ENTRIES_A_COLUMN]
+        picked3 = keep.tile([P, PACK, V], BF16, name="picked3", align_bytes=64)
+        for j in range(PACK):
+            nc.scalar.activation(picked3[:, j, :], planes[j][:].indirect(last_piece), COPY)
         for j in range(PACK - 1):
-            gather(j, 0, S)
+            gather(j, 0, S - V)
         weave(nc.scalar.copy, x_grouped[:, :, 0:2], 0, 2, 0, LEAD)
+        weave(nc.vector.tensor_copy, piece2_grouped[:, :, 0:2], 0, 2, LEAD, S - V)
         gather(PACK - 1, 0, LEAD)
-        gather(PACK - 1, LEAD, S)
+        gather(PACK - 1, LEAD, S - V)
         weave(nc.vector.tensor_copy, x_grouped[:, :, 2:4], 2, 4, 0, LEAD)
+        weave(nc.vector.tensor_copy, piece2_grouped[:, :, 2:4], 2, 4, LEAD, S - V)
 
+        piece3_grouped = keep.tile([P, V, PACK], BF16, name="piece3_grouped", align_bytes=64)
+        nc.scalar.copy(
+            piece3_grouped[:].rearrange("p (c i) j -> p c j i", i=4), picked3[:].rearrange("p j (c i) -> p c j i", i=4)
+        )
 
-        def w_views(h, first, last, first_t, last_t):
-            dst = w_grouped[:, first_t:last_t, h * W_HALF + first : h * W_HALF + last, :].rearrange("p t m j -> p m j t")
-            src = w_raw[h][:].rearrange("p j (m t) -> p m j t", t=PACK)[:, first:last, :, first_t:last_t]
-            return dst, src
-
-        nc.scalar.copy(*w_views(0, 0, W_HALF, 0, PACK))
-        nc.vector.tensor_copy(*w_views(1, 0, W_HALF, 0, 2))
-        nc.scalar.copy(*w_views(1, 0, W_HALF, 2, PACK))
-
-        lead_codes = shared.tile([P, LEAD], U32, name="lead_codes", align_bytes=64, offset=0)
+        lead_codes = keep.tile([P, LEAD], U32, name="lead_codes", align_bytes=64)
         lead_scales = keep.tile([P, LEAD], U8, name="lead_scales", align_bytes=64)
         quantize(lead_codes[:], lead_scales[:], x_grouped[:])
 
+        def w_views(h, first, last, first_t, last_t):
+            start = w_places[h][0]
+            dst = w_grouped[:, first_t:last_t, first:last, :].rearrange("p t m j -> p m j t")
+            src = w_raw[h][:].rearrange("p j (m t) -> p m j t", t=PACK)[:, first - start : last - start, :, first_t:last_t]
+            return dst, src
+
+        nc.vector.tensor_copy(*w_views(0, W_SCALAR, W_FIRST, 0, PACK))
+        for u in range(2):
+            nc.scalar.copy(*w_views(0, 0, W_SCALAR, 2 * u, 2 * u + 2))
+            nc.vector.tensor_copy(*w_views(1, W_FIRST, P, 2 * u, 2 * u + 2))
+
         w_codes = [keep.tile([P, P], U32, name="w_codes%d" % t, align_bytes=64) for t in range(PACK)]
         w_scales = [keep.tile([P, P], U8, name="w_scales%d" % t, align_bytes=64) for t in range(PACK)]
-        late_grouped = (
-            shared.tile([P, V, PACK], BF16, name="piece2_grouped", align_bytes=64, offset=4 * LEAD),
-            keep.tile([P, V, PACK], BF16, name="piece3_grouped", tag="w_raw1", align_bytes=64),
-        )
-        for d in (2, 3):
-            weave(nc.scalar.copy, late_grouped[d - 2][:, :, 0:2], 0, 2, d * V, (d + 1) * V)
         for t in range(PACK):
-            if t == 3:
-                weave(nc.vector.tensor_copy, late_grouped[0][:, :, 2:4], 2, 4, LEAD, S - V)
             quantize(w_codes[t][:], w_scales[t][:], w_grouped[:, t, :, :])
 
         late = {}
-        for d in (2, 3):
-            if d == 3:
-                weave(nc.vector.tensor_copy, late_grouped[1][:, :, 2:4], 2, 4, S - V, S)
-            codes = keep.tile([P, V], U32, name="piece%d_codes" % d, align_bytes=64)
+        late_codes = (
+            shared.tile([P, V], U32, name="piece2_codes", align_bytes=64, offset=0),
+            shared.tile([P, V], U32, name="piece3_codes", align_bytes=64, offset=4 * V),
+        )
+        for d, grouped in ((2, piece2_grouped), (3, piece3_grouped)):
             scales = keep.tile([P, V], U8, name="piece%d_scales" % d, align_bytes=64)
-            quantize(codes[:], scales[:], late_grouped[d - 2][:])
-            late[d] = (codes[:], scales[:])
+            quantize(late_codes[d - 2][:], scales[:], grouped[:])
+            late[d] = (late_codes[d - 2][:], scales[:])
 
         def multiply(out, t, codes, scales):
             nc.tensor.matmul_mx(

@@ -20,15 +20,13 @@ MULT = mybir.AluOpType.mult
 
 ENTRIES_A_COLUMN = 16
 LEAD = 2 * V
-W_FIRST = 88
-W_SCALAR = 72
+W_PLACES = ((0, 64), (64, 96), (96, 128))
 
 
 def tile_picked_andpool_none_lo_kernel(tc, xT, w1, offs, out_0, out_1, out_2):
     nc = tc.nc
     with ExitStack() as ctx:
         keep = ctx.enter_context(tc.tile_pool(name="keep", bufs=1))
-        shared = ctx.enter_context(tc.tile_pool(name="shared", bufs=1))
         psum = ctx.enter_context(tc.psum_pool(name="psum", bufs=1))
 
         warm_in = keep.tile([P, 1], F32, name="warm_in")
@@ -40,21 +38,20 @@ def tile_picked_andpool_none_lo_kernel(tc, xT, w1, offs, out_0, out_1, out_2):
         w_rows = w1.rearrange("(p j) c -> p j c", j=PACK)
         offsets = keep.tile([P, S // ENTRIES_A_COLUMN], U16, name="offsets")
         planes = [keep.tile([P, T], F32, name="plane%d" % j) for j in range(PACK)]
-        w_places = ((0, W_FIRST), (W_FIRST, P))
         w_raw = [
-            shared.tile([P, PACK, PACK * W_FIRST], F32, name="w_raw0", align_bytes=64, offset=0),
-            keep.tile([P, PACK, PACK * (P - W_FIRST)], F32, name="w_raw1", align_bytes=64),
+            keep.tile([P, PACK, PACK * (last - first)], F32, name="w_raw%d" % h, tag="w_raw%d" % h, align_bytes=64)
+            for h, (first, last) in enumerate(W_PLACES)
         ]
 
         nc.sync.dma_start(planes[0][:], x_rows[:, 0, :])
         nc.sync.dma_start(offsets[:], offs)
         for j in range(1, PACK):
             nc.sync.dma_start(planes[j][:], x_rows[:, j, :])
-        for h in range(2):
-            nc.sync.dma_start(w_raw[h][:], w_rows[:, :, PACK * w_places[h][0] : PACK * w_places[h][1]])
+        for h, (first, last) in enumerate(W_PLACES):
+            nc.sync.dma_start(w_raw[h][:], w_rows[:, :, PACK * first : PACK * last])
 
         w_grouped = keep.tile([P, PACK, P, PACK], BF16, name="w_grouped", align_bytes=64)
-        picked = keep.tile([P, PACK, S - V], BF16, name="picked", align_bytes=64)
+        picked = keep.tile([P, PACK, S], BF16, name="picked", align_bytes=64)
         x_grouped = keep.tile([P, LEAD, PACK], BF16, name="x_grouped", align_bytes=64)
 
         def gather(j, lo, hi):
@@ -67,54 +64,56 @@ def tile_picked_andpool_none_lo_kernel(tc, xT, w1, offs, out_0, out_1, out_2):
         def quantize(codes, scales, grouped):
             nc.vector.quantize_mx(out=codes.bitcast(FP8X4), scales=scales, in_=grouped.rearrange("p n j -> p (n j)"))
 
-        piece2_grouped = keep.tile([P, V, PACK], BF16, name="piece2_grouped", align_bytes=64)
-        last_piece = offsets[:, (S - V) // ENTRIES_A_COLUMN : S // ENTRIES_A_COLUMN]
-        picked3 = keep.tile([P, PACK, V], BF16, name="picked3", align_bytes=64)
-        for j in range(PACK):
-            nc.scalar.activation(picked3[:, j, :], planes[j][:].indirect(last_piece), COPY)
+        def scalar_gather(j, lo, hi):
+            columns = offsets[:, lo // ENTRIES_A_COLUMN : hi // ENTRIES_A_COLUMN]
+            nc.scalar.activation(picked[:, j, lo:hi], planes[j][:].indirect(columns), COPY)
+
         for j in range(PACK - 1):
             gather(j, 0, S - V)
+            scalar_gather(j, S - V, S)
         weave(nc.scalar.copy, x_grouped[:, :, 0:2], 0, 2, 0, LEAD)
-        weave(nc.vector.tensor_copy, piece2_grouped[:, :, 0:2], 0, 2, LEAD, S - V)
-        gather(PACK - 1, 0, LEAD)
-        gather(PACK - 1, LEAD, S - V)
-        weave(nc.vector.tensor_copy, x_grouped[:, :, 2:4], 2, 4, 0, LEAD)
-        weave(nc.vector.tensor_copy, piece2_grouped[:, :, 2:4], 2, 4, LEAD, S - V)
-
-        piece3_grouped = keep.tile([P, V, PACK], BF16, name="piece3_grouped", align_bytes=64)
-        nc.scalar.copy(
-            piece3_grouped[:].rearrange("p (c i) j -> p c j i", i=4), picked3[:].rearrange("p j (c i) -> p c j i", i=4)
-        )
-
+        scalar_gather(PACK - 1, LEAD, S)
+        lead_pieces = [slice(d * V, (d + 1) * V) for d in range(2)]
+        for piece in lead_pieces:
+            gather(PACK - 1, piece.start, piece.stop)
+        for piece in lead_pieces:
+            weave(nc.vector.tensor_copy, x_grouped[:, piece, 2:4], 2, 4, piece.start, piece.stop)
         lead_codes = keep.tile([P, LEAD], U32, name="lead_codes", align_bytes=64)
         lead_scales = keep.tile([P, LEAD], U8, name="lead_scales", align_bytes=64)
-        quantize(lead_codes[:], lead_scales[:], x_grouped[:])
+        for piece in lead_pieces:
+            quantize(lead_codes[:, piece], lead_scales[:, piece], x_grouped[:, piece, :])
 
-        def w_views(h, first, last, first_t, last_t):
-            start = w_places[h][0]
+        def w_views(h, first_t, last_t):
+            first, last = W_PLACES[h]
             dst = w_grouped[:, first_t:last_t, first:last, :].rearrange("p t m j -> p m j t")
-            src = w_raw[h][:].rearrange("p j (m t) -> p m j t", t=PACK)[:, first - start : last - start, :, first_t:last_t]
+            src = w_raw[h][:].rearrange("p j (m t) -> p m j t", t=PACK)[:, :, :, first_t:last_t]
             return dst, src
 
-        nc.vector.tensor_copy(*w_views(0, W_SCALAR, W_FIRST, 0, PACK))
+        nc.scalar.copy(*w_views(0, 0, PACK))
+        nc.vector.tensor_copy(*w_views(1, 0, PACK))
         for u in range(2):
-            nc.scalar.copy(*w_views(0, 0, W_SCALAR, 2 * u, 2 * u + 2))
-            nc.vector.tensor_copy(*w_views(1, W_FIRST, P, 2 * u, 2 * u + 2))
+            nc.vector.tensor_copy(*w_views(2, 2 * u, 2 * u + 2))
 
         w_codes = [keep.tile([P, P], U32, name="w_codes%d" % t, align_bytes=64) for t in range(PACK)]
         w_scales = [keep.tile([P, P], U8, name="w_scales%d" % t, align_bytes=64) for t in range(PACK)]
         for t in range(PACK):
             quantize(w_codes[t][:], w_scales[t][:], w_grouped[:, t, :, :])
 
+        def weave_whole(copy, d, tag):
+            grouped = keep.tile([P, V, PACK], BF16, name="piece%d_grouped" % d, tag=tag, align_bytes=64)
+            copy(
+                grouped[:].rearrange("p (c i) j -> p c j i", i=4),
+                picked[:, :, d * V : (d + 1) * V].rearrange("p j (c i) -> p c j i", i=4),
+            )
+            return grouped
+
         late = {}
-        late_codes = (
-            shared.tile([P, V], U32, name="piece2_codes", align_bytes=64, offset=0),
-            shared.tile([P, V], U32, name="piece3_codes", align_bytes=64, offset=4 * V),
-        )
-        for d, grouped in ((2, piece2_grouped), (3, piece3_grouped)):
+        for d, copy, tag in ((2, nc.scalar.copy, "w_raw0"), (3, nc.vector.tensor_copy, "w_raw2")):
+            grouped = weave_whole(copy, d, tag)
+            codes = keep.tile([P, V], U32, name="piece%d_codes" % d, align_bytes=64)
             scales = keep.tile([P, V], U8, name="piece%d_scales" % d, align_bytes=64)
-            quantize(late_codes[d - 2][:], scales[:], grouped[:])
-            late[d] = (late_codes[d - 2][:], scales[:])
+            quantize(codes[:], scales[:], grouped[:])
+            late[d] = (codes[:], scales[:])
 
         def multiply(out, t, codes, scales):
             nc.tensor.matmul_mx(

@@ -90,26 +90,26 @@ def tile_picked_andpool_none_lo_kernel(tc, xT, w1, offs, out_0, out_1, out_2):
             return dst, src
 
         nc.scalar.copy(*w_views(0, 0, PACK))
-        nc.vector.tensor_copy(*w_views(1, 0, PACK))
-        for u in range(2):
-            nc.vector.tensor_copy(*w_views(2, 2 * u, 2 * u + 2))
+        for h in (1, 2):
+            for u in range(2):
+                nc.vector.tensor_copy(*w_views(h, 2 * u, 2 * u + 2))
 
         w_codes = [keep.tile([P, P], U32, name="w_codes%d" % t, align_bytes=64) for t in range(PACK)]
         w_scales = [keep.tile([P, P], U8, name="w_scales%d" % t, align_bytes=64) for t in range(PACK)]
         for t in range(PACK):
             quantize(w_codes[t][:], w_scales[t][:], w_grouped[:, t, :, :])
 
-        def weave_whole(copy, d, tag):
-            grouped = keep.tile([P, V, PACK], BF16, name="piece%d_grouped" % d, tag=tag, align_bytes=64)
-            copy(
-                grouped[:].rearrange("p (c i) j -> p c j i", i=4),
-                picked[:, :, d * V : (d + 1) * V].rearrange("p j (c i) -> p c j i", i=4),
-            )
-            return grouped
+        piece2_grouped = keep.tile([P, V, PACK], BF16, name="piece2_grouped", tag="w_raw0", align_bytes=64)
+        nc.scalar.copy(
+            piece2_grouped[:].rearrange("p (c i) j -> p c j i", i=4),
+            picked[:, :, LEAD : S - V].rearrange("p j (c i) -> p c j i", i=4),
+        )
+        piece3_grouped = keep.tile([P, V, PACK], BF16, name="piece3_grouped", tag="w_raw2", align_bytes=64)
 
         late = {}
-        for d, copy, tag in ((2, nc.scalar.copy, "w_raw0"), (3, nc.vector.tensor_copy, "w_raw2")):
-            grouped = weave_whole(copy, d, tag)
+        for d, grouped in ((2, piece2_grouped), (3, piece3_grouped)):
+            if d == 3:
+                weave(nc.vector.tensor_copy, grouped[:], 0, PACK, S - V, S)
             codes = keep.tile([P, V], U32, name="piece%d_codes" % d, align_bytes=64)
             scales = keep.tile([P, V], U8, name="piece%d_scales" % d, align_bytes=64)
             quantize(codes[:], scales[:], grouped[:])

@@ -100,10 +100,7 @@ def tile_picked_andpool_none_lo_kernel(tc, xT, w1, offs, out_0, out_1, out_2):
             quantize(w_codes[t][:], w_scales[t][:], w_grouped[:, t, :, :])
 
         piece2_grouped = keep.tile([P, V, PACK], BF16, name="piece2_grouped", tag="w_raw0", align_bytes=64)
-        nc.scalar.copy(
-            piece2_grouped[:].rearrange("p (c i) j -> p c j i", i=4),
-            picked[:, :, LEAD : S - V].rearrange("p j (c i) -> p c j i", i=4),
-        )
+        weave(nc.scalar.copy, piece2_grouped[:], 0, PACK, LEAD, S - V)
         piece3_grouped = keep.tile([P, V, PACK], BF16, name="piece3_grouped", tag="w_raw2", align_bytes=64)
 
         late = {}

@@ -20,13 +20,15 @@ MULT = mybir.AluOpType.mult
 
 ENTRIES_A_COLUMN = 16
 LEAD = 2 * V
-W_PLACES = ((0, 64), (64, 96), (96, 128))
+W_HALF = P // 2
+W_VECTOR_FIRST, W_VECTOR_LAST = 34, (44, 32)
 
 
 def tile_picked_andpool_none_lo_kernel(tc, xT, w1, offs, out_0, out_1, out_2):
     nc = tc.nc
     with ExitStack() as ctx:
         keep = ctx.enter_context(tc.tile_pool(name="keep", bufs=1))
+        shared = ctx.enter_context(tc.tile_pool(name="shared", bufs=1))
         psum = ctx.enter_context(tc.psum_pool(name="psum", bufs=1))
 
         warm_in = keep.tile([P, 1], F32, name="warm_in")
@@ -39,16 +41,16 @@ def tile_picked_andpool_none_lo_kernel(tc, xT, w1, offs, out_0, out_1, out_2):
         offsets = keep.tile([P, S // ENTRIES_A_COLUMN], U16, name="offsets")
         planes = [keep.tile([P, T], F32, name="plane%d" % j) for j in range(PACK)]
         w_raw = [
-            keep.tile([P, PACK, PACK * (last - first)], F32, name="w_raw%d" % h, tag="w_raw%d" % h, align_bytes=64)
-            for h, (first, last) in enumerate(W_PLACES)
+            keep.tile([P, PACK, N // 2], F32, name="w_raw0", align_bytes=64),
+            shared.tile([P, PACK, N // 2], F32, name="w_raw1", align_bytes=64, offset=0),
         ]
 
         nc.sync.dma_start(planes[0][:], x_rows[:, 0, :])
         nc.sync.dma_start(offsets[:], offs)
         for j in range(1, PACK):
             nc.sync.dma_start(planes[j][:], x_rows[:, j, :])
-        for h, (first, last) in enumerate(W_PLACES):
-            nc.sync.dma_start(w_raw[h][:], w_rows[:, :, PACK * first : PACK * last])
+        for h in range(2):
+            nc.sync.dma_start(w_raw[h][:], w_rows[:, :, h * (N // 2) : (h + 1) * (N // 2)])
 
         w_grouped = keep.tile([P, PACK, P, PACK], BF16, name="w_grouped", align_bytes=64)
         picked = keep.tile([P, PACK, S], BF16, name="picked", align_bytes=64)
@@ -83,31 +85,31 @@ def tile_picked_andpool_none_lo_kernel(tc, xT, w1, offs, out_0, out_1, out_2):
         for piece in lead_pieces:
             quantize(lead_codes[:, piece], lead_scales[:, piece], x_grouped[:, piece, :])
 
-        def w_views(h, first_t, last_t):
-            first, last = W_PLACES[h]
-            dst = w_grouped[:, first_t:last_t, first:last, :].rearrange("p t m j -> p m j t")
-            src = w_raw[h][:].rearrange("p j (m t) -> p m j t", t=PACK)[:, :, :, first_t:last_t]
+        piece2_grouped = keep.tile([P, V, PACK], BF16, name="piece2_grouped", align_bytes=64)
+        weave(nc.scalar.copy, piece2_grouped[:], 0, PACK, LEAD, S - V)
+
+        def w_views(h, first, last, first_t, last_t):
+            dst = w_grouped[:, first_t:last_t, h * W_HALF + first : h * W_HALF + last, :].rearrange("p t m j -> p m j t")
+            src = w_raw[h][:].rearrange("p j (m t) -> p m j t", t=PACK)[:, first:last, :, first_t:last_t]
             return dst, src
 
-        nc.scalar.copy(*w_views(0, 0, PACK))
-        for h in (1, 2):
-            for u in range(2):
-                nc.vector.tensor_copy(*w_views(h, 2 * u, 2 * u + 2))
+        nc.scalar.copy(*w_views(0, W_VECTOR_FIRST, W_HALF, 0, PACK))
+        for u in range(2):
+            nc.vector.tensor_copy(*w_views(0, 0, W_VECTOR_FIRST, 2 * u, 2 * u + 2))
+        for u in range(2):
+            nc.vector.tensor_copy(*w_views(1, 0, W_VECTOR_LAST[u], 2 * u, 2 * u + 2))
+            nc.scalar.copy(*w_views(1, W_VECTOR_LAST[u], W_HALF, 2 * u, 2 * u + 2))
 
         w_codes = [keep.tile([P, P], U32, name="w_codes%d" % t, align_bytes=64) for t in range(PACK)]
         w_scales = [keep.tile([P, P], U8, name="w_scales%d" % t, align_bytes=64) for t in range(PACK)]
         for t in range(PACK):
             quantize(w_codes[t][:], w_scales[t][:], w_grouped[:, t, :, :])
 
-        piece2_grouped = keep.tile([P, V, PACK], BF16, name="piece2_grouped", tag="w_raw0", align_bytes=64)
-        weave(nc.scalar.copy, piece2_grouped[:], 0, PACK, LEAD, S - V)
-        piece3_grouped = keep.tile([P, V, PACK], BF16, name="piece3_grouped", tag="w_raw2", align_bytes=64)
-
+        piece3_grouped = shared.tile([P, V, PACK], BF16, name="piece3_grouped", align_bytes=64, offset=0)
+        weave(nc.scalar.copy, piece3_grouped[:], 0, PACK, S - V, S)
         late = {}
         for d, grouped in ((2, piece2_grouped), (3, piece3_grouped)):
-            if d == 3:
-                weave(nc.vector.tensor_copy, grouped[:], 0, PACK, S - V, S)
-            codes = keep.tile([P, V], U32, name="piece%d_codes" % d, align_bytes=64)
+            codes = shared.tile([P, V], U32, name="piece%d_codes" % d, align_bytes=64, offset=1024 * (d - 1))
             scales = keep.tile([P, V], U8, name="piece%d_scales" % d, align_bytes=64)
             quantize(codes[:], scales[:], grouped[:])
             late[d] = (codes[:], scales[:])

@@ -39,10 +39,10 @@ def tile_picked_andpool_none_lo_kernel(tc, xT, w1, offs, out_0, out_1, out_2):
         x_rows = xT.rearrange("(p j) t -> p j t", j=PACK)
         w_rows = w1.rearrange("(p j) c -> p j c", j=PACK)
         offsets = keep.tile([P, S // ENTRIES_A_COLUMN], U16, name="offsets")
-        planes = [keep.tile([P, T], F32, name="plane%d" % j) for j in range(PACK)]
+        planes = [keep.tile([P, T], F32, name="plane%d" % j, align_bytes=256) for j in range(PACK)]
         w_raw = [
-            keep.tile([P, PACK, N // 2], F32, name="w_raw0", align_bytes=64),
-            shared.tile([P, PACK, N // 2], F32, name="w_raw1", align_bytes=64, offset=0),
+            keep.tile([P, PACK, N // 2], F32, name="w_raw0", align_bytes=256),
+            shared.tile([P, PACK, N // 2], F32, name="w_raw1", align_bytes=256, offset=0),
         ]
 
         nc.sync.dma_start(planes[0][:], x_rows[:, 0, :])
@@ -52,9 +52,9 @@ def tile_picked_andpool_none_lo_kernel(tc, xT, w1, offs, out_0, out_1, out_2):
         for h in range(2):
             nc.sync.dma_start(w_raw[h][:], w_rows[:, :, h * (N // 2) : (h + 1) * (N // 2)])
 
-        w_grouped = keep.tile([P, PACK, P, PACK], BF16, name="w_grouped", align_bytes=64)
-        picked = keep.tile([P, PACK, S], BF16, name="picked", align_bytes=64)
-        x_grouped = keep.tile([P, LEAD, PACK], BF16, name="x_grouped", align_bytes=64)
+        w_grouped = keep.tile([P, PACK, P, PACK], BF16, name="w_grouped", align_bytes=256)
+        picked = keep.tile([P, PACK, S], BF16, name="picked", align_bytes=256)
+        x_grouped = keep.tile([P, LEAD, PACK], BF16, name="x_grouped", align_bytes=256)
 
         def gather(j, lo, hi):
             columns = offsets[:, lo // ENTRIES_A_COLUMN : hi // ENTRIES_A_COLUMN]
@@ -80,12 +80,12 @@ def tile_picked_andpool_none_lo_kernel(tc, xT, w1, offs, out_0, out_1, out_2):
             gather(PACK - 1, piece.start, piece.stop)
         for piece in lead_pieces:
             weave(nc.vector.tensor_copy, x_grouped[:, piece, 2:4], 2, 4, piece.start, piece.stop)
-        lead_codes = keep.tile([P, LEAD], U32, name="lead_codes", align_bytes=64)
-        lead_scales = keep.tile([P, LEAD], U8, name="lead_scales", align_bytes=64)
+        lead_codes = keep.tile([P, LEAD], U32, name="lead_codes", align_bytes=256)
+        lead_scales = keep.tile([P, LEAD], U8, name="lead_scales", align_bytes=256)
         for piece in lead_pieces:
             quantize(lead_codes[:, piece], lead_scales[:, piece], x_grouped[:, piece, :])
 
-        piece2_grouped = keep.tile([P, V, PACK], BF16, name="piece2_grouped", align_bytes=64)
+        piece2_grouped = keep.tile([P, V, PACK], BF16, name="piece2_grouped", align_bytes=256)
         weave(nc.scalar.copy, piece2_grouped[:], 0, PACK, LEAD, S - V)
 
         def w_views(h, first, last, first_t, last_t):
@@ -100,17 +100,17 @@ def tile_picked_andpool_none_lo_kernel(tc, xT, w1, offs, out_0, out_1, out_2):
             nc.vector.tensor_copy(*w_views(1, 0, W_VECTOR_LAST[u], 2 * u, 2 * u + 2))
             nc.scalar.copy(*w_views(1, W_VECTOR_LAST[u], W_HALF, 2 * u, 2 * u + 2))
 
-        w_codes = [keep.tile([P, P], U32, name="w_codes%d" % t, align_bytes=64) for t in range(PACK)]
-        w_scales = [keep.tile([P, P], U8, name="w_scales%d" % t, align_bytes=64) for t in range(PACK)]
+        w_codes = [keep.tile([P, P], U32, name="w_codes%d" % t, align_bytes=256) for t in range(PACK)]
+        w_scales = [keep.tile([P, P], U8, name="w_scales%d" % t, align_bytes=256) for t in range(PACK)]
         for t in range(PACK):
             quantize(w_codes[t][:], w_scales[t][:], w_grouped[:, t, :, :])
 
-        piece3_grouped = shared.tile([P, V, PACK], BF16, name="piece3_grouped", align_bytes=64, offset=0)
+        piece3_grouped = shared.tile([P, V, PACK], BF16, name="piece3_grouped", align_bytes=256, offset=0)
         weave(nc.scalar.copy, piece3_grouped[:], 0, PACK, S - V, S)
         late = {}
         for d, grouped in ((2, piece2_grouped), (3, piece3_grouped)):
-            codes = shared.tile([P, V], U32, name="piece%d_codes" % d, align_bytes=64, offset=1024 * (d - 1))
-            scales = keep.tile([P, V], U8, name="piece%d_scales" % d, align_bytes=64)
+            codes = shared.tile([P, V], U32, name="piece%d_codes" % d, align_bytes=256, offset=1024 * (d - 1))
+            scales = keep.tile([P, V], U8, name="piece%d_scales" % d, align_bytes=256)
             quantize(codes[:], scales[:], grouped[:])
             late[d] = (codes[:], scales[:])
 
@@ -143,7 +143,7 @@ def tile_picked_andpool_none_lo_kernel(tc, xT, w1, offs, out_0, out_1, out_2):
             nc.scalar.activation(truth[:], bank[:], SIGMOID)
             return truth
 
-        y_grouped = keep.tile([P, V, PACK], BF16, name="y_grouped", align_bytes=64)
+        y_grouped = keep.tile([P, V, PACK], BF16, name="y_grouped", align_bytes=256)
         two_pieces = [lead_product(u) for u in range(2)]
         three_pieces = []
         for u in range(2):
@@ -154,7 +154,7 @@ def tile_picked_andpool_none_lo_kernel(tc, xT, w1, offs, out_0, out_1, out_2):
 
         v_halves = (slice(0, V // 2), slice(V // 2, V))
         truth = truth_values(0, 3)
-        result0 = keep.tile([P, 2, V], F32, name="result0")
+        result0 = keep.tile([P, 2, V], F32, name="result0", align_bytes=256)
         for part in v_halves:
             nc.vector.tensor_tensor(result0[:, :, part], three_pieces[0][:, :, part], truth[:, :, part], MULT)
 
@@ -165,7 +165,7 @@ def tile_picked_andpool_none_lo_kernel(tc, xT, w1, offs, out_0, out_1, out_2):
             truth[:].rearrange("p e v -> p v e"),
             MULT,
         )
-        result1 = keep.tile([P, 2, V], F32, name="result1")
+        result1 = keep.tile([P, 2, V], F32, name="result1", align_bytes=256)
         nc.vector.tensor_tensor(result1[:], three_pieces[1][:], truth[:], MULT)
 
         out_rows = out_0.rearrange("(p t) v -> p t v", t=PACK)
@@ -174,8 +174,8 @@ def tile_picked_andpool_none_lo_kernel(tc, xT, w1, offs, out_0, out_1, out_2):
         for part in v_halves:
             nc.scalar.copy(y_grouped[:, part, 0:2], result0[:, :, part].rearrange("p e v -> p v e"))
 
-        y_codes = keep.tile([P, V], U32, name="y_codes", align_bytes=64)
-        y_scales = keep.tile([P, V], U8, name="y_scales", align_bytes=64)
+        y_codes = keep.tile([P, V], U32, name="y_codes", align_bytes=256)
+        y_scales = keep.tile([P, V], U8, name="y_scales", align_bytes=256)
         quantize(y_codes[:], y_scales[:], y_grouped[:])
         nc.sync.dma_start(out_1.rearrange("z l c r -> (z l) (c r)").bitcast(I32), y_codes[:].bitcast(I32))
         scale_rows = out_2.rearrange("z q c -> (z q) c").bitcast(I32)

@@ -21,7 +21,7 @@ MULT = mybir.AluOpType.mult
 ENTRIES_A_COLUMN = 16
 LEAD = 2 * V
 W_HALF = P // 2
-W_VECTOR_FIRST, W_VECTOR_LAST = 34, (44, 32)
+W_VECTOR_FIRST, W_VECTOR_LAST = 32, (40, 32)
 
 
 def tile_picked_andpool_none_lo_kernel(tc, xT, w1, offs, out_0, out_1, out_2):
@@ -85,33 +85,36 @@ def tile_picked_andpool_none_lo_kernel(tc, xT, w1, offs, out_0, out_1, out_2):
         for piece in lead_pieces:
             quantize(lead_codes[:, piece], lead_scales[:, piece], x_grouped[:, piece, :])
 
-        piece2_grouped = keep.tile([P, V, PACK], BF16, name="piece2_grouped", align_bytes=256)
-        weave(nc.scalar.copy, piece2_grouped[:], 0, PACK, LEAD, S - V)
-
         def w_views(h, first, last, first_t, last_t):
             dst = w_grouped[:, first_t:last_t, h * W_HALF + first : h * W_HALF + last, :].rearrange("p t m j -> p m j t")
             src = w_raw[h][:].rearrange("p j (m t) -> p m j t", t=PACK)[:, first:last, :, first_t:last_t]
             return dst, src
 
-        nc.scalar.copy(*w_views(0, W_VECTOR_FIRST, W_HALF, 0, PACK))
-        for u in range(2):
-            nc.vector.tensor_copy(*w_views(0, 0, W_VECTOR_FIRST, 2 * u, 2 * u + 2))
+        nc.scalar.copy(*w_views(0, 0, W_HALF, 0, 2))
+        nc.vector.tensor_copy(*w_views(0, 0, W_VECTOR_FIRST, 2, PACK))
+        nc.scalar.copy(*w_views(0, W_VECTOR_FIRST, W_HALF, 2, PACK))
         for u in range(2):
             nc.vector.tensor_copy(*w_views(1, 0, W_VECTOR_LAST[u], 2 * u, 2 * u + 2))
             nc.scalar.copy(*w_views(1, W_VECTOR_LAST[u], W_HALF, 2 * u, 2 * u + 2))
 
         w_codes = [keep.tile([P, P], U32, name="w_codes%d" % t, align_bytes=256) for t in range(PACK)]
         w_scales = [keep.tile([P, P], U8, name="w_scales%d" % t, align_bytes=256) for t in range(PACK)]
-        for t in range(PACK):
+        for places in (slice(0, W_HALF), slice(W_HALF, P)):
+            quantize(w_codes[0][:, places], w_scales[0][:, places], w_grouped[:, 0, places, :])
+        for t in range(1, PACK):
             quantize(w_codes[t][:], w_scales[t][:], w_grouped[:, t, :, :])
 
-        piece3_grouped = shared.tile([P, V, PACK], BF16, name="piece3_grouped", align_bytes=256, offset=0)
-        weave(nc.scalar.copy, piece3_grouped[:], 0, PACK, S - V, S)
+        late_grouped = [
+            shared.tile([P, V, PACK], BF16, name="piece%d_grouped" % d, align_bytes=256, offset=1024 * (d - 2))
+            for d in (2, 3)
+        ]
+        weave(nc.scalar.copy, late_grouped[0][:], 0, PACK, LEAD, S - V)
+        weave(nc.vector.tensor_copy, late_grouped[1][:], 0, PACK, S - V, S)
         late = {}
-        for d, grouped in ((2, piece2_grouped), (3, piece3_grouped)):
-            codes = shared.tile([P, V], U32, name="piece%d_codes" % d, align_bytes=256, offset=1024 * (d - 1))
+        for d in (2, 3):
+            codes = keep.tile([P, V], U32, name="piece%d_codes" % d, align_bytes=256)
             scales = keep.tile([P, V], U8, name="piece%d_scales" % d, align_bytes=256)
-            quantize(codes[:], scales[:], grouped[:])
+            quantize(codes[:], scales[:], late_grouped[d - 2][:])
             late[d] = (codes[:], scales[:])
 
         def multiply(out, t, codes, scales):

@@ -49,8 +49,9 @@ def tile_picked_andpool_none_lo_kernel(tc, xT, w1, offs, out_0, out_1, out_2):
         nc.sync.dma_start(offsets[:], offs)
         for j in range(1, PACK):
             nc.sync.dma_start(planes[j][:], x_rows[:, j, :])
-        for h in range(2):
-            nc.sync.dma_start(w_raw[h][:], w_rows[:, :, h * (N // 2) : (h + 1) * (N // 2)])
+        nc.sync.dma_start(w_raw[0][:], w_rows[:, :, 0 : N // 2])
+        for slots in (slice(0, 2), slice(2, 3), slice(3, PACK)):
+            nc.sync.dma_start(w_raw[1][:, slots, :], w_rows[:, slots, N // 2 : N])
 
         w_grouped = keep.tile([P, PACK, P, PACK], BF16, name="w_grouped", align_bytes=256)
         picked = keep.tile([P, PACK, S], BF16, name="picked", align_bytes=256)

@@ -20,6 +20,7 @@ MULT = mybir.AluOpType.mult
 
 ENTRIES_A_COLUMN = 16
 LEAD = 2 * V
+RUN = 4
 W_HALF = P // 2
 W_VECTOR_FIRST, W_VECTOR_LAST = 32, (40, 32)
 
@@ -62,7 +63,10 @@ def tile_picked_andpool_none_lo_kernel(tc, xT, w1, offs, out_0, out_1, out_2):
             nc.vector.tensor_copy(picked[:, j, lo:hi], planes[j][:].indirect(columns))
 
         def weave(copy, into, first_plane, last_plane, lo, hi):
-            copy(into, picked[:, first_plane:last_plane, lo:hi].rearrange("p j n -> p n j"))
+            copy(
+                into.rearrange("p (c i) j -> p c j i", i=RUN),
+                picked[:, first_plane:last_plane, lo:hi].rearrange("p j (c i) -> p c j i", i=RUN),
+            )
 
         def quantize(codes, scales, grouped):
             nc.vector.quantize_mx(out=codes.bitcast(FP8X4), scales=scales, in_=grouped.rearrange("p n j -> p (n j)"))
@@ -164,9 +168,9 @@ def tile_picked_andpool_none_lo_kernel(tc, xT, w1, offs, out_0, out_1, out_2):
 
         truth = truth_values(1, 3)
         nc.vector.tensor_tensor(
-            y_grouped[:, :, 2:4],
-            three_pieces[1][:].rearrange("p e v -> p v e"),
-            truth[:].rearrange("p e v -> p v e"),
+            y_grouped[:, :, 2:4].rearrange("p (c i) e -> p c e i", i=2),
+            three_pieces[1][:].rearrange("p e (c i) -> p c e i", i=2),
+            truth[:].rearrange("p e (c i) -> p c e i", i=2),
             MULT,
         )
         result1 = keep.tile([P, 2, V], F32, name="result1", align_bytes=256)
@@ -176,7 +180,10 @@ def tile_picked_andpool_none_lo_kernel(tc, xT, w1, offs, out_0, out_1, out_2):
         for u, result in enumerate((result0, result1)):
             nc.sync.dma_start(out_rows[:, 2 * u : 2 * u + 2, :], result[:])
         for part in v_halves:
-            nc.scalar.copy(y_grouped[:, part, 0:2], result0[:, :, part].rearrange("p e v -> p v e"))
+            nc.scalar.copy(
+                y_grouped[:, part, 0:2].rearrange("p (c i) e -> p c e i", i=2),
+                result0[:, :, part].rearrange("p e (c i) -> p c e i", i=2),
+            )
 
         y_codes = keep.tile([P, V], U32, name="y_codes", align_bytes=256)
         y_scales = keep.tile([P, V], U8, name="y_scales", align_bytes=256)

@@ -19,8 +19,10 @@ COPY = mybir.ActivationFunctionType.Copy
 MULT = mybir.AluOpType.mult
 
 ENTRIES_A_COLUMN = 16
+PIECE_BYTES = V * PACK * 2
 LEAD = 2 * V
-RUN = 4
+WEAVE_RUN = 4
+V_RUN = 2
 W_HALF = P // 2
 W_VECTOR_FIRST, W_VECTOR_LAST = 32, (40, 32)
 
@@ -37,8 +39,8 @@ def tile_picked_andpool_none_lo_kernel(tc, xT, w1, offs, out_0, out_1, out_2):
         nc.vector.memset(warm_in[:], 0.0)
         nc.scalar.activation(warm_out[:], warm_in[:], SIGMOID)
 
-        x_rows = xT.rearrange("(p j) t -> p j t", j=PACK)
-        w_rows = w1.rearrange("(p j) c -> p j c", j=PACK)
+        x_rows = xT.rearrange("(q j b) t -> j q b t", j=PACK, b=2)
+        w_rows = w1.rearrange("(q j b) c -> b q j c", j=PACK, b=2)
         offsets = keep.tile([P, S // ENTRIES_A_COLUMN], U16, name="offsets")
         planes = [keep.tile([P, T], F32, name="plane%d" % j, align_bytes=256) for j in range(PACK)]
         w_raw = [
@@ -46,26 +48,26 @@ def tile_picked_andpool_none_lo_kernel(tc, xT, w1, offs, out_0, out_1, out_2):
             shared.tile([P, PACK, N // 2], F32, name="w_raw1", align_bytes=256, offset=0),
         ]
 
-        nc.sync.dma_start(planes[0][:], x_rows[:, 0, :])
+        nc.sync.dma_start(planes[0][:], x_rows[0])
         nc.sync.dma_start(offsets[:], offs)
         for j in range(1, PACK):
-            nc.sync.dma_start(planes[j][:], x_rows[:, j, :])
-        nc.sync.dma_start(w_raw[0][:], w_rows[:, :, 0 : N // 2])
-        for slots in (slice(0, 2), slice(2, 3), slice(3, PACK)):
-            nc.sync.dma_start(w_raw[1][:, slots, :], w_rows[:, slots, N // 2 : N])
+            nc.sync.dma_start(planes[j][:], x_rows[j])
+        for h in range(2):
+            for b in range(2):
+                nc.sync.dma_start(w_raw[h][b:P:2, :, :], w_rows[b][:, :, h * (N // 2) : (h + 1) * (N // 2)])
 
         w_grouped = keep.tile([P, PACK, P, PACK], BF16, name="w_grouped", align_bytes=256)
         picked = keep.tile([P, PACK, S], BF16, name="picked", align_bytes=256)
         x_grouped = keep.tile([P, LEAD, PACK], BF16, name="x_grouped", align_bytes=256)
 
-        def gather(j, lo, hi):
+        def vector_gather(j, lo, hi):
             columns = offsets[:, lo // ENTRIES_A_COLUMN : hi // ENTRIES_A_COLUMN]
             nc.vector.tensor_copy(picked[:, j, lo:hi], planes[j][:].indirect(columns))
 
         def weave(copy, into, first_plane, last_plane, lo, hi):
             copy(
-                into.rearrange("p (c i) j -> p c j i", i=RUN),
-                picked[:, first_plane:last_plane, lo:hi].rearrange("p j (c i) -> p c j i", i=RUN),
+                into.rearrange("p (c i) j -> p c j i", i=WEAVE_RUN),
+                picked[:, first_plane:last_plane, lo:hi].rearrange("p j (c i) -> p c j i", i=WEAVE_RUN),
             )
 
         def quantize(codes, scales, grouped):
@@ -76,13 +78,13 @@ def tile_picked_andpool_none_lo_kernel(tc, xT, w1, offs, out_0, out_1, out_2):
             nc.scalar.activation(picked[:, j, lo:hi], planes[j][:].indirect(columns), COPY)
 
         for j in range(PACK - 1):
-            gather(j, 0, S - V)
+            vector_gather(j, 0, S - V)
             scalar_gather(j, S - V, S)
         weave(nc.scalar.copy, x_grouped[:, :, 0:2], 0, 2, 0, LEAD)
         scalar_gather(PACK - 1, LEAD, S)
         lead_pieces = [slice(d * V, (d + 1) * V) for d in range(2)]
         for piece in lead_pieces:
-            gather(PACK - 1, piece.start, piece.stop)
+            vector_gather(PACK - 1, piece.start, piece.stop)
         for piece in lead_pieces:
             weave(nc.vector.tensor_copy, x_grouped[:, piece, 2:4], 2, 4, piece.start, piece.stop)
         lead_codes = keep.tile([P, LEAD], U32, name="lead_codes", align_bytes=256)
@@ -110,7 +112,7 @@ def tile_picked_andpool_none_lo_kernel(tc, xT, w1, offs, out_0, out_1, out_2):
             quantize(w_codes[t][:], w_scales[t][:], w_grouped[:, t, :, :])
 
         late_grouped = [
-            shared.tile([P, V, PACK], BF16, name="piece%d_grouped" % d, align_bytes=256, offset=1024 * (d - 2))
+            shared.tile([P, V, PACK], BF16, name="piece%d_grouped" % d, align_bytes=256, offset=PIECE_BYTES * (d - 2))
             for d in (2, 3)
         ]
         weave(nc.scalar.copy, late_grouped[0][:], 0, PACK, LEAD, S - V)
@@ -168,9 +170,9 @@ def tile_picked_andpool_none_lo_kernel(tc, xT, w1, offs, out_0, out_1, out_2):
 
         truth = truth_values(1, 3)
         nc.vector.tensor_tensor(
-            y_grouped[:, :, 2:4].rearrange("p (c i) e -> p c e i", i=2),
-            three_pieces[1][:].rearrange("p e (c i) -> p c e i", i=2),
-            truth[:].rearrange("p e (c i) -> p c e i", i=2),
+            y_grouped[:, :, 2:4].rearrange("p (c i) e -> p c e i", i=V_RUN),
+            three_pieces[1][:].rearrange("p e (c i) -> p c e i", i=V_RUN),
+            truth[:].rearrange("p e (c i) -> p c e i", i=V_RUN),
             MULT,
         )
         result1 = keep.tile([P, 2, V], F32, name="result1", align_bytes=256)
@@ -181,8 +183,8 @@ def tile_picked_andpool_none_lo_kernel(tc, xT, w1, offs, out_0, out_1, out_2):
             nc.sync.dma_start(out_rows[:, 2 * u : 2 * u + 2, :], result[:])
         for part in v_halves:
             nc.scalar.copy(
-                y_grouped[:, part, 0:2].rearrange("p (c i) e -> p c e i", i=2),
-                result0[:, :, part].rearrange("p e (c i) -> p c e i", i=2),
+                y_grouped[:, part, 0:2].rearrange("p (c i) e -> p c e i", i=V_RUN),
+                result0[:, :, part].rearrange("p e (c i) -> p c e i", i=V_RUN),
             )
 
         y_codes = keep.tile([P, V], U32, name="y_codes", align_bytes=256)

from contextlib import ExitStack

import concourse.mybir as mybir

K, T, S, V, N = 512, 1024, 512, 128, 512
P = 128
PACK = 4
FLOPS = 2 * K * N * S

F32 = mybir.dt.float32
BF16 = mybir.dt.bfloat16
I32 = mybir.dt.int32
U32 = mybir.dt.uint32
U16 = mybir.dt.uint16
U8 = mybir.dt.uint8
FP8X4 = mybir.dt.float8_e4m3fn_x4
SIGMOID = mybir.ActivationFunctionType.Sigmoid
COPY = mybir.ActivationFunctionType.Copy
MULT = mybir.AluOpType.mult

ENTRIES_A_COLUMN = 16
PIECE_BYTES = V * PACK * 2
LEAD = 2 * V
WEAVE_RUN = 4
V_RUN = 2
W_HALF = P // 2
W_VECTOR_FIRST, W_VECTOR_LAST = 32, (40, 32)


def tile_picked_andpool_none_lo_kernel(tc, xT, w1, offs, out_0, out_1, out_2):
    nc = tc.nc
    with ExitStack() as ctx:
        keep = ctx.enter_context(tc.tile_pool(name="keep", bufs=1))
        shared = ctx.enter_context(tc.tile_pool(name="shared", bufs=1))
        psum = ctx.enter_context(tc.psum_pool(name="psum", bufs=1))

        warm_in = keep.tile([P, 1], F32, name="warm_in")
        warm_out = keep.tile([P, 1], F32, name="warm_out")
        nc.vector.memset(warm_in[:], 0.0)
        nc.scalar.activation(warm_out[:], warm_in[:], SIGMOID)

        x_rows = xT.rearrange("(q j b) t -> j q b t", j=PACK, b=2)
        w_rows = w1.rearrange("(q j b) c -> b q j c", j=PACK, b=2)
        offsets = keep.tile([P, S // ENTRIES_A_COLUMN], U16, name="offsets")
        planes = [keep.tile([P, T], F32, name="plane%d" % j, align_bytes=256) for j in range(PACK)]
        w_raw = [
            keep.tile([P, PACK, N // 2], F32, name="w_raw0", align_bytes=256),
            shared.tile([P, PACK, N // 2], F32, name="w_raw1", align_bytes=256, offset=0),
        ]

        nc.sync.dma_start(planes[0][:], x_rows[0])
        nc.sync.dma_start(offsets[:], offs)
        for j in range(1, PACK):
            nc.sync.dma_start(planes[j][:], x_rows[j])
        for h in range(2):
            for b in range(2):
                nc.sync.dma_start(w_raw[h][b:P:2, :, :], w_rows[b][:, :, h * (N // 2) : (h + 1) * (N // 2)])

        w_grouped = keep.tile([P, PACK, P, PACK], BF16, name="w_grouped", align_bytes=256)
        picked = keep.tile([P, PACK, S], BF16, name="picked", align_bytes=256)
        x_grouped = keep.tile([P, LEAD, PACK], BF16, name="x_grouped", align_bytes=256)

        def vector_gather(j, lo, hi):
            columns = offsets[:, lo // ENTRIES_A_COLUMN : hi // ENTRIES_A_COLUMN]
            nc.vector.tensor_copy(picked[:, j, lo:hi], planes[j][:].indirect(columns))

        def weave(copy, into, first_plane, last_plane, lo, hi):
            copy(
                into.rearrange("p (c i) j -> p c j i", i=WEAVE_RUN),
                picked[:, first_plane:last_plane, lo:hi].rearrange("p j (c i) -> p c j i", i=WEAVE_RUN),
            )

        def quantize(codes, scales, grouped):
            nc.vector.quantize_mx(out=codes.bitcast(FP8X4), scales=scales, in_=grouped.rearrange("p n j -> p (n j)"))

        def scalar_gather(j, lo, hi):
            columns = offsets[:, lo // ENTRIES_A_COLUMN : hi // ENTRIES_A_COLUMN]
            nc.scalar.activation(picked[:, j, lo:hi], planes[j][:].indirect(columns), COPY)

        for j in range(PACK - 1):
            vector_gather(j, 0, S - V)
            scalar_gather(j, S - V, S)
        weave(nc.scalar.copy, x_grouped[:, :, 0:2], 0, 2, 0, LEAD)
        scalar_gather(PACK - 1, LEAD, S)
        lead_pieces = [slice(d * V, (d + 1) * V) for d in range(2)]
        for piece in lead_pieces:
            vector_gather(PACK - 1, piece.start, piece.stop)
        for piece in lead_pieces:
            weave(nc.vector.tensor_copy, x_grouped[:, piece, 2:4], 2, 4, piece.start, piece.stop)
        lead_codes = keep.tile([P, LEAD], U32, name="lead_codes", align_bytes=256)
        lead_scales = keep.tile([P, LEAD], U8, name="lead_scales", align_bytes=256)
        for piece in lead_pieces:
            quantize(lead_codes[:, piece], lead_scales[:, piece], x_grouped[:, piece, :])

        def w_views(h, first, last, first_t, last_t):
            dst = w_grouped[:, first_t:last_t, h * W_HALF + first : h * W_HALF + last, :].rearrange("p t m j -> p m j t")
            src = w_raw[h][:].rearrange("p j (m t) -> p m j t", t=PACK)[:, first:last, :, first_t:last_t]
            return dst, src

        nc.scalar.copy(*w_views(0, 0, W_HALF, 0, 2))
        nc.vector.tensor_copy(*w_views(0, 0, W_VECTOR_FIRST, 2, PACK))
        nc.scalar.copy(*w_views(0, W_VECTOR_FIRST, W_HALF, 2, PACK))
        for u in range(2):
            nc.vector.tensor_copy(*w_views(1, 0, W_VECTOR_LAST[u], 2 * u, 2 * u + 2))
            nc.scalar.copy(*w_views(1, W_VECTOR_LAST[u], W_HALF, 2 * u, 2 * u + 2))

        w_codes = [keep.tile([P, P], U32, name="w_codes%d" % t, align_bytes=256) for t in range(PACK)]
        w_scales = [keep.tile([P, P], U8, name="w_scales%d" % t, align_bytes=256) for t in range(PACK)]
        for places in (slice(0, W_HALF), slice(W_HALF, P)):
            quantize(w_codes[0][:, places], w_scales[0][:, places], w_grouped[:, 0, places, :])
        for t in range(1, PACK):
            quantize(w_codes[t][:], w_scales[t][:], w_grouped[:, t, :, :])

        late_grouped = [
            shared.tile([P, V, PACK], BF16, name="piece%d_grouped" % d, align_bytes=256, offset=PIECE_BYTES * (d - 2))
            for d in (2, 3)
        ]
        weave(nc.scalar.copy, late_grouped[0][:], 0, PACK, LEAD, S - V)
        weave(nc.vector.tensor_copy, late_grouped[1][:], 0, PACK, S - V, S)
        late = {}
        for d in (2, 3):
            codes = keep.tile([P, V], U32, name="piece%d_codes" % d, align_bytes=256)
            scales = keep.tile([P, V], U8, name="piece%d_scales" % d, align_bytes=256)
            quantize(codes[:], scales[:], late_grouped[d - 2][:])
            late[d] = (codes[:], scales[:])

        def multiply(out, t, codes, scales):
            nc.tensor.matmul_mx(
                out=out,
                lhsT=w_codes[t][:].bitcast(FP8X4),
                lhsT_scale=w_scales[t][:],
                rhs=codes.bitcast(FP8X4),
                rhs_scale=scales,
                start=True,
                stop=True,
            )

        def lead_product(u):
            truth = keep.tile([P, 2, 2, V], F32, name="lead_truth%d" % u)
            for e in range(2):
                bank = psum.tile([P, LEAD], F32, name="lead_bank%d%d" % (u, e))
                multiply(bank[:], 2 * u + e, lead_codes[:], lead_scales[:])
                nc.scalar.activation(truth[:, e, :, :].rearrange("p d v -> p (d v)"), bank[:], SIGMOID)
            product = keep.tile([P, 2, V], F32, name="lead_product%d" % u)
            nc.vector.tensor_tensor(product[:], truth[:, :, 0, :], truth[:, :, 1, :], MULT)
            return product

        def truth_values(u, d):
            bank = psum.tile([P, 2, V], F32, name="bank%d%d" % (u, d))
            for e in range(2):
                multiply(bank[:, e, :], 2 * u + e, *late[d])
            truth = keep.tile([P, 2, V], F32, name="truth%d%d" % (u, d))
            nc.scalar.activation(truth[:], bank[:], SIGMOID)
            return truth

        y_grouped = keep.tile([P, V, PACK], BF16, name="y_grouped", align_bytes=256)
        two_pieces = [lead_product(u) for u in range(2)]
        three_pieces = []
        for u in range(2):
            truth = truth_values(u, 2)
            product = keep.tile([P, 2, V], F32, name="three_pieces%d" % u)
            nc.vector.tensor_tensor(product[:], two_pieces[u][:], truth[:], MULT)
            three_pieces.append(product)

        v_halves = (slice(0, V // 2), slice(V // 2, V))
        truth = truth_values(0, 3)
        result0 = keep.tile([P, 2, V], F32, name="result0", align_bytes=256)
        for part in v_halves:
            nc.vector.tensor_tensor(result0[:, :, part], three_pieces[0][:, :, part], truth[:, :, part], MULT)

        truth = truth_values(1, 3)
        nc.vector.tensor_tensor(
            y_grouped[:, :, 2:4].rearrange("p (c i) e -> p c e i", i=V_RUN),
            three_pieces[1][:].rearrange("p e (c i) -> p c e i", i=V_RUN),
            truth[:].rearrange("p e (c i) -> p c e i", i=V_RUN),
            MULT,
        )
        result1 = keep.tile([P, 2, V], F32, name="result1", align_bytes=256)
        nc.vector.tensor_tensor(result1[:], three_pieces[1][:], truth[:], MULT)

        out_rows = out_0.rearrange("(p t) v -> p t v", t=PACK)
        for u, result in enumerate((result0, result1)):
            nc.sync.dma_start(out_rows[:, 2 * u : 2 * u + 2, :], result[:])
        for part in v_halves:
            nc.scalar.copy(
                y_grouped[:, part, 0:2].rearrange("p (c i) e -> p c e i", i=V_RUN),
                result0[:, :, part].rearrange("p e (c i) -> p c e i", i=V_RUN),
            )

        y_codes = keep.tile([P, V], U32, name="y_codes", align_bytes=256)
        y_scales = keep.tile([P, V], U8, name="y_scales", align_bytes=256)
        quantize(y_codes[:], y_scales[:], y_grouped[:])
        nc.sync.dma_start(out_1.rearrange("z l c r -> (z l) (c r)").bitcast(I32), y_codes[:].bitcast(I32))
        scale_rows = out_2.rearrange("z q c -> (z q) c").bitcast(I32)
        for q in range(4):
            queue = nc.sync if q % 2 == 0 else nc.scalar
            queue.dma_start(scale_rows[4 * q : 4 * q + 4, :], y_scales[32 * q : 32 * q + 4, :].bitcast(I32))
